import numpy as np
import ml_dtypes


def mxq(x, axis, fmt="e4m3"):
    dtype, down = {"e4m3": (ml_dtypes.float8_e4m3fn, 7), "e5m2": (ml_dtypes.float8_e5m2, 14)}[fmt]
    v = np.moveaxis(np.asarray(x, np.float32).astype(ml_dtypes.bfloat16).astype(np.float64), axis, -1)
    blocks = v.reshape(v.shape[:-1] + (-1, 32))
    amax = np.abs(blocks).max(-1, keepdims=True)
    byte = np.maximum(np.where(amax > 0, np.frexp(amax)[1] - 1 + 127, 0) - down, 1)
    scale = np.exp2(byte - 127.0)
    codes = (blocks / scale).astype(np.float32).astype(dtype).astype(np.float64)
    return np.moveaxis((codes * scale).reshape(v.shape), -1, axis)


WIDE = False


def mx_kscale(k):
    if not WIDE:
        return np.ones(k)
    levels = np.array([10, -10, 5, -5, 0])
    if k % 512:
        return np.exp2(np.random.permutation(np.resize(levels, k // 32))).repeat(32)
    a = np.empty((k // 512, 16))
    for p in range(k // 512):
        a[p, :8] = np.random.permutation(np.resize(levels, 8))
        for g in range(8):
            far = levels[np.abs(levels - a[p, g]) >= 10]
            a[p, g + 8] = far[np.random.randint(len(far))]
    return np.exp2(a.ravel()).repeat(32)


def f64(x):
    return np.asarray(x).astype(np.float64)


def striped(idx):
    return np.tile(idx.reshape(-1, 16).T, (8, 1)).astype(np.uint16)


def unstriped(offs):
    return offs[:16].T.reshape(-1).astype(np.int64)


def pack_weight(w):
    k, n = w.shape
    w = f64(np.asarray(w, np.float32).astype(ml_dtypes.bfloat16)).reshape(k // 32, 32, n)
    amax = np.abs(w).max(1)
    byte = np.clip(np.where(amax > 0, np.frexp(amax)[1] - 1 + 127 - 7, 1), 1, 254)
    scaled = (w * np.exp2(127.0 - byte)[:, None, :]).reshape(k, n).astype(np.float32)
    words = np.ascontiguousarray(scaled.reshape(k // 512, 128, 4, n).transpose(0, 1, 3, 2)).astype(ml_dtypes.float8_e4m3fn).view(np.uint8)
    return words, np.ascontiguousarray(byte.astype(np.uint8).reshape(k // 512, 16, n))


def unpack_weight(words, scales):
    g, p, n, _ = words.shape
    vals = np.ascontiguousarray(words).view(ml_dtypes.float8_e4m3fn).astype(np.float64) * np.repeat(np.exp2(scales.astype(np.float64) - 127.0), 8, axis=1)[..., None]
    return vals.transpose(0, 1, 3, 2).reshape(g * 512, n)


K, T, S, N, U = 1024, 2048, 1024, 128, 1024


def setup_inputs():
    n = np.random.standard_normal
    s = mx_kscale(K)[:, None]
    packed_xT = pack_weight(n((K, T)) * s)
    return {
        "x_words": packed_xT[0],
        "x_scales": packed_xT[1],
        "w1": (n((K, N)) / np.sqrt(K) / s).astype(np.float32),
        "w2": (n((K, N)) / np.sqrt(K) / s).astype(np.float32),
        "w3": (n((K, N)) / np.sqrt(K) / s).astype(np.float32),
        "offs": striped(np.random.permutation(T)[:S]),
        "src": striped(np.random.permutation(S)[(S * np.random.uniform(0, 1, U) ** 4).astype(np.int64)]),
        "dst": striped(np.random.permutation(S)),
    }


def reference(x_words, x_scales, w1, w2, w3, offs, src, dst):
    xq = unpack_weight(x_words, x_scales)[:, unstriped(offs)]
    y = mxq(f64(w1), 0, "e4m3").T @ xq
    e = mxq(f64(w2), 0, "e4m3").T @ xq
    h = mxq(f64(w3), 0, "e4m3").T @ xq
    return (np.tanh(y[:, unstriped(dst)] + e[:, unstriped(src)])) * h[:, unstriped(src)]

@@ -1,0 +1,164 @@
+from contextlib import ExitStack
+
+import concourse.mybir as mybir
+
+K, T, S, N, U = 1024, 2048, 1024, 128, 1024
+FLOPS = 3 * 2 * K * N * S
+
+F32 = mybir.dt.float32
+BF16 = mybir.dt.bfloat16
+I32 = mybir.dt.int32
+U32 = mybir.dt.uint32
+U16 = mybir.dt.uint16
+U8 = mybir.dt.uint8
+FP8X4 = mybir.dt.float8_e4m3fn_x4
+ADD = mybir.AluOpType.add
+MULT = mybir.AluOpType.mult
+TANH = mybir.ActivationFunctionType.Tanh
+
+P = 128
+PACK = 4
+K_PASS = P * PACK
+PASSES = K // K_PASS
+GROUP = 16
+HALF = 512
+Y_PIECES = ((0, 512), (512, 768), (768, 1024))
+HALVES = ((0, 512), (512, 1024))
+EDGE_PIECES = ((0, 512), (512, 768), (768, 1024))
+
+
+def tile_picked_edgeatt_tanh_p_kernel(tc, x_words, x_scales, w1, w2, w3, offs, src, dst, out):
+    nc = tc.nc
+    with ExitStack() as ctx:
+        keep = ctx.enter_context(tc.tile_pool(name="keep", bufs=1))
+        psum = ctx.enter_context(tc.psum_pool(name="psum", bufs=1))
+
+        def sb(name, shape, dtype, tag=None):
+            return keep.tile(shape, dtype, name=name, tag=tag or name, align_bytes=64)
+
+        def entries(lst, a, b):
+            return lst[:, a // GROUP : b // GROUP]
+
+        offs_sb = keep.tile([P, S // GROUP], U16, name="offs_sb")
+        src_sb = keep.tile([P, U // GROUP], U16, name="src_sb")
+        dst_sb = keep.tile([P, U // GROUP], U16, name="dst_sb")
+        scale_tab = sb("scale_tab", [P, T], U8)
+        word_tab = [sb("word_tab%d" % z, [P, T], U32) for z in range(PASSES)]
+        w_raw = [sb("w_raw%d" % i, [P, PASSES, PACK * N], F32) for i in range(3)]
+        w_code = [sb("w_code%d" % i, [P, PASSES * N], U32) for i in range(3)]
+        w_scale = [sb("w_scale%d" % i, [P, PASSES * N], U8) for i in range(3)]
+        w1_grp = [sb("w1_grp%d" % z, [P, N * PACK], BF16) for z in range(PASSES)]
+        w2_grp = sb("w2_grp", [P, PASSES * N * PACK], BF16)
+        w3_grp = sb("w3_grp", [P, PASSES * N * PACK], BF16)
+        weights = (w1, w2, w3)
+
+        def load_words(z):
+            nc.sync.dma_start(out=word_tab[z][:].bitcast(I32), in_=x_words[z].rearrange("p n t -> p (n t)").bitcast(I32))
+
+        def load_weight(i, z):
+            nc.sync.dma_start(out=w_raw[i][:, z, :], in_=weights[i][z * K_PASS : (z + 1) * K_PASS, :].rearrange("(p j) m -> p (j m)", j=PACK))
+
+        nc.vector.memset(scale_tab[:].bitcast(I32), 0)
+        nc.sync.dma_start(offs_sb[:], offs)
+        nc.sync.dma_start(dst_sb[:], dst)
+        nc.sync.dma_start(src_sb[:], src)
+        for q in range(4):
+            nc.sync.dma_start(out=scale_tab[32 * q : 32 * q + 4 * PASSES, :].bitcast(I32), in_=x_scales[:, 4 * q : 4 * q + 4, :].bitcast(I32))
+        load_words(0)
+        load_weight(0, 0)
+        load_words(1)
+        load_weight(0, 1)
+        for i in (1, 2):
+            for z in range(PASSES):
+                load_weight(i, z)
+
+        def interleave(grouped, i, z):
+            nc.scalar.copy(
+                out=grouped.rearrange("p (c i t) -> p c t i", i=4, t=PACK),
+                in_=w_raw[i][:, z, :].rearrange("p (t c i) -> p c t i", i=4, t=PACK),
+            )
+
+        def quantise(grouped, i, a, b):
+            nc.vector.quantize_mx(out=w_code[i][:, a:b].bitcast(FP8X4), scales=w_scale[i][:, a:b], in_=grouped)
+
+        scale_pick = sb("scale_pick", [P, S], U8)
+        first_pick = sb("first_pick", [P, S], U32)
+        nc.vector.tensor_copy(scale_pick[:], scale_tab[:].indirect(offs_sb[:]))
+        nc.vector.tensor_copy(first_pick[:], word_tab[0][:].indirect(offs_sb[:]))
+        second_pick = []
+
+        def picked(z, a, b):
+            if z == 0:
+                return first_pick[:, a:b]
+            return second_pick[a // HALF][:, a % HALF : a % HALF + b - a]
+
+        def pick_second(a, b):
+            nc.vector.tensor_copy(picked(1, a, b), word_tab[1][:].indirect(entries(offs_sb, a, b)))
+
+        banks = {}
+
+        def product(i, z, a, b):
+            if z == 0:
+                banks[i, a] = psum.tile([P, b - a], F32, name="acc%d_%d" % (i, a))
+            nc.tensor.matmul_mx(
+                out=banks[i, a][:],
+                lhsT=w_code[i][:, z * N : (z + 1) * N].bitcast(FP8X4),
+                lhsT_scale=w_scale[i][:, z * N : (z + 1) * N],
+                rhs=picked(z, a, b).bitcast(FP8X4),
+                rhs_scale=scale_pick[4 * z :, a:b],
+                start=(z == 0),
+                stop=(z == PASSES - 1),
+            )
+
+        interleave(w1_grp[0][:], 0, 0)
+        quantise(w1_grp[0][:], 0, 0, N)
+        for a, b in Y_PIECES:
+            product(0, 0, a, b)
+        second_pick.append(sb("second_pick0", [P, HALF], U32))
+        pick_second(0, HALF)
+        interleave(w1_grp[1][:], 0, 1)
+        quantise(w1_grp[1][:], 0, N, 2 * N)
+        product(0, 1, 0, HALF)
+        second_pick.append(sb("second_pick1", [P, HALF], U32, tag="w1_grp1"))
+        for a, b in Y_PIECES[1:]:
+            pick_second(a, b)
+            product(0, 1, a, b)
+
+        for z in range(PASSES):
+            interleave(w2_grp[:, z * K_PASS : (z + 1) * K_PASS], 1, z)
+        quantise(w2_grp[:], 1, 0, 2 * N)
+        y = sb("y", [P, S], F32, tag="w_raw1")
+        for a, b in Y_PIECES[:-1]:
+            nc.scalar.copy(out=y[:, a:b], in_=banks[0, a][:])
+        a, b = Y_PIECES[-1]
+        nc.vector.tensor_copy(out=y[:, a:b], in_=banks[0, a][:])
+        for a, b in HALVES:
+            for z in range(PASSES):
+                product(1, z, a, b)
+
+        y_dst = [sb("y_dst0", [P, HALF], F32, tag="w2_grp")]
+        nc.vector.tensor_copy(y_dst[0][:], y[:].indirect(entries(dst_sb, 0, HALF)))
+        for z in range(PASSES):
+            interleave(w3_grp[:, z * K_PASS : (z + 1) * K_PASS], 2, z)
+        quantise(w3_grp[:], 2, 0, 2 * N)
+        y_dst.append(sb("y_dst1", [P, HALF], F32, tag="w3_grp"))
+        nc.vector.tensor_copy(y_dst[1][:], y[:].indirect(entries(dst_sb, HALF, U)))
+
+        e = sb("e", [P, S], F32)
+        h = sb("h", [P, S], F32)
+        for a, b in HALVES:
+            nc.scalar.copy(out=e[:, a:b], in_=banks[1, a][:])
+        for a, b in HALVES:
+            for z in range(PASSES):
+                product(2, z, a, b)
+            nc.scalar.copy(out=h[:, a:b], in_=banks[2, a][:])
+
+        pre = sb("pre", [P, U], F32)
+        gate = sb("gate", [P, U], F32, tag="scale_pick")
+        msg = sb("msg", [P, U], F32)
+        for a, b in EDGE_PIECES:
+            nc.vector.tensor_tensor(pre[:, a:b], e[:].indirect(entries(src_sb, a, b)), y_dst[a // HALF][:, a % HALF : a % HALF + b - a], ADD)
+            nc.scalar.activation(gate[:, a:b], pre[:, a:b], TANH)
+        for a, b in EDGE_PIECES:
+            nc.vector.tensor_tensor(msg[:, a:b], h[:].indirect(entries(src_sb, a, b)), gate[:, a:b], MULT)
+            nc.sync.dma_start(out=out[:, a:b], in_=msg[:, a:b])

@@ -22,9 +22,10 @@ K_PASS = P * PACK
 PASSES = K // K_PASS
 GROUP = 16
 HALF = 512
-Y_PIECES = ((0, 512), (512, 768), (768, 1024))
+PICK_PIECES = ((512, 768), (768, 1024))
+Y_PIECES = ((0, 512), (512, 768), (768, 896), (896, 1024))
 HALVES = ((0, 512), (512, 1024))
-EDGE_PIECES = ((0, 512), (512, 768), (768, 1024))
+EDGE_PIECES = ((0, 512), (512, 896), (896, 1024))
 
 
 def tile_picked_edgeatt_tanh_p_kernel(tc, x_words, x_scales, w1, w2, w3, offs, src, dst, out):
@@ -120,18 +121,20 @@ def tile_picked_edgeatt_tanh_p_kernel(tc, x_words, x_scales, w1, w2, w3, offs, s
         quantise(w1_grp[1][:], 0, N, 2 * N)
         product(0, 1, 0, HALF)
         second_pick.append(sb("second_pick1", [P, HALF], U32, tag="w1_grp1"))
-        for a, b in Y_PIECES[1:]:
+        for a, b in PICK_PIECES:
             pick_second(a, b)
-            product(0, 1, a, b)
+            for c, d in Y_PIECES:
+                if a <= c < b:
+                    product(0, 1, c, d)
 
         for z in range(PASSES):
             interleave(w2_grp[:, z * K_PASS : (z + 1) * K_PASS], 1, z)
         quantise(w2_grp[:], 1, 0, 2 * N)
         y = sb("y", [P, S], F32, tag="w_raw1")
-        for a, b in Y_PIECES[:-1]:
+        for a, b in Y_PIECES[0::2]:
             nc.scalar.copy(out=y[:, a:b], in_=banks[0, a][:])
-        a, b = Y_PIECES[-1]
-        nc.vector.tensor_copy(out=y[:, a:b], in_=banks[0, a][:])
+        for a, b in Y_PIECES[1::2]:
+            nc.vector.tensor_copy(out=y[:, a:b], in_=banks[0, a][:])
         for a, b in HALVES:
             for z in range(PASSES):
                 product(1, z, a, b)
@@ -156,8 +159,8 @@ def tile_picked_edgeatt_tanh_p_kernel(tc, x_words, x_scales, w1, w2, w3, offs, s
         pre = sb("pre", [P, U], F32)
         gate = sb("gate", [P, U], F32, tag="scale_pick")
         msg = sb("msg", [P, U], F32)
-        for a, b in EDGE_PIECES:
-            nc.vector.tensor_tensor(pre[:, a:b], e[:].indirect(entries(src_sb, a, b)), y_dst[a // HALF][:, a % HALF : a % HALF + b - a], ADD)
+        for a, b in HALVES:
+            nc.vector.tensor_tensor(pre[:, a:b], e[:].indirect(entries(src_sb, a, b)), y_dst[a // HALF][:], ADD)
             nc.scalar.activation(gate[:, a:b], pre[:, a:b], TANH)
         for a, b in EDGE_PIECES:
             nc.vector.tensor_tensor(msg[:, a:b], h[:].indirect(entries(src_sb, a, b)), gate[:, a:b], MULT)

@@ -62,9 +62,11 @@ def tile_picked_edgeatt_tanh_p_kernel(tc, x_words, x_scales, w1, w2, w3, offs, s
         nc.vector.memset(scale_tab[:].bitcast(I32), 0)
         nc.sync.dma_start(offs_sb[:], offs)
         nc.sync.dma_start(dst_sb[:], dst)
-        nc.sync.dma_start(src_sb[:], src)
-        for q in range(4):
+        for q in range(2):
             nc.sync.dma_start(out=scale_tab[32 * q : 32 * q + 4 * PASSES, :].bitcast(I32), in_=x_scales[:, 4 * q : 4 * q + 4, :].bitcast(I32))
+            for z in range(PASSES):
+                row = 32 * (q + 2) + 4 * z
+                nc.sync.dma_start(out=scale_tab[row : row + 4, :].bitcast(I32), in_=x_scales[z, 4 * (q + 2) : 4 * (q + 2) + 4, :].bitcast(I32))
         load_words(0)
         load_weight(0, 0)
         load_words(1)
@@ -72,6 +74,7 @@ def tile_picked_edgeatt_tanh_p_kernel(tc, x_words, x_scales, w1, w2, w3, offs, s
         for i in (1, 2):
             for z in range(PASSES):
                 load_weight(i, z)
+        nc.sync.dma_start(src_sb[:], src)
 
         def interleave(grouped, i, z):
             nc.scalar.copy(

@@ -22,6 +22,7 @@ K_PASS = P * PACK
 PASSES = K // K_PASS
 GROUP = 16
 HALF = 512
+ROW0 = 24
 PICK_PIECES = ((512, 768), (768, 1024))
 Y_PIECES = ((0, 512), (512, 768), (768, 896), (896, 1024))
 HALVES = ((0, 512), (512, 1024))
@@ -32,10 +33,14 @@ def tile_picked_edgeatt_tanh_p_kernel(tc, x_words, x_scales, w1, w2, w3, offs, s
     nc = tc.nc
     with ExitStack() as ctx:
         keep = ctx.enter_context(tc.tile_pool(name="keep", bufs=1))
+        reuse = ctx.enter_context(tc.tile_pool(name="reuse", bufs=1))
         psum = ctx.enter_context(tc.psum_pool(name="psum", bufs=1))
 
         def sb(name, shape, dtype, tag=None):
             return keep.tile(shape, dtype, name=name, tag=tag or name, align_bytes=64)
+
+        def at(name, shape, dtype, offset):
+            return reuse.tile(shape, dtype, name=name, align_bytes=64, offset=offset)
 
         def entries(lst, a, b):
             return lst[:, a // GROUP : b // GROUP]
@@ -44,8 +49,9 @@ def tile_picked_edgeatt_tanh_p_kernel(tc, x_words, x_scales, w1, w2, w3, offs, s
         src_sb = keep.tile([P, U // GROUP], U16, name="src_sb")
         dst_sb = keep.tile([P, U // GROUP], U16, name="dst_sb")
         scale_tab = sb("scale_tab", [P, T], U8)
-        word_tab = [sb("word_tab%d" % z, [P, T], U32) for z in range(PASSES)]
-        w_raw = [sb("w_raw%d" % i, [P, PASSES, PACK * N], F32) for i in range(3)]
+        scale_pick = sb("scale_pick", [P, S], U8)
+        word_tab = [at("word_tab0", [P, T], U32, 4096), sb("word_tab1", [P, T], U32)]
+        w_raw = {(0, 0): at("w1_raw0", [P, PACK * N], F32, 512)}
         w_code = [sb("w_code%d" % i, [P, PASSES * N], U32) for i in range(3)]
         w_scale = [sb("w_scale%d" % i, [P, PASSES * N], U8) for i in range(3)]
         w1_grp = [sb("w1_grp%d" % z, [P, N * PACK], BF16) for z in range(PASSES)]
@@ -57,37 +63,34 @@ def tile_picked_edgeatt_tanh_p_kernel(tc, x_words, x_scales, w1, w2, w3, offs, s
             nc.sync.dma_start(out=word_tab[z][:].bitcast(I32), in_=x_words[z].rearrange("p n t -> p (n t)").bitcast(I32))
 
         def load_weight(i, z):
-            nc.sync.dma_start(out=w_raw[i][:, z, :], in_=weights[i][z * K_PASS : (z + 1) * K_PASS, :].rearrange("(p j) m -> p (j m)", j=PACK))
+            nc.sync.dma_start(out=w_raw[i, z][:], in_=weights[i][z * K_PASS : (z + 1) * K_PASS, :].rearrange("(p j) m -> p (j m)", j=PACK))
 
-        nc.vector.memset(scale_tab[:].bitcast(I32), 0)
         nc.sync.dma_start(offs_sb[:], offs)
-        nc.sync.dma_start(dst_sb[:], dst)
-        for q in range(2):
-            nc.sync.dma_start(out=scale_tab[32 * q : 32 * q + 4 * PASSES, :].bitcast(I32), in_=x_scales[:, 4 * q : 4 * q + 4, :].bitcast(I32))
-            for z in range(PASSES):
-                row = 32 * (q + 2) + 4 * z
-                nc.sync.dma_start(out=scale_tab[row : row + 4, :].bitcast(I32), in_=x_scales[z, 4 * (q + 2) : 4 * (q + 2) + 4, :].bitcast(I32))
+        for q in range(4):
+            nc.vector.memset(scale_tab[32 * q : 32 * q + ROW0, :].bitcast(I32), 0)
+            nc.sync.dma_start(out=scale_tab[32 * q + ROW0 : 32 * q + 32, :].bitcast(I32), in_=x_scales[:, 4 * q : 4 * q + 4, :].bitcast(I32))
         load_words(0)
         load_weight(0, 0)
-        load_words(1)
-        load_weight(0, 1)
-        for i in (1, 2):
-            for z in range(PASSES):
-                load_weight(i, z)
+        nc.sync.dma_start(dst_sb[:], dst)
         nc.sync.dma_start(src_sb[:], src)
+        load_words(1)
 
         def interleave(grouped, i, z):
             nc.scalar.copy(
                 out=grouped.rearrange("p (c i t) -> p c t i", i=4, t=PACK),
-                in_=w_raw[i][:, z, :].rearrange("p (t c i) -> p c t i", i=4, t=PACK),
+                in_=w_raw[i, z][:].rearrange("p (t c i) -> p c t i", i=4, t=PACK),
             )
 
         def quantise(grouped, i, a, b):
             nc.vector.quantize_mx(out=w_code[i][:, a:b].bitcast(FP8X4), scales=w_scale[i][:, a:b], in_=grouped)
 
-        scale_pick = sb("scale_pick", [P, S], U8)
+        scale_rows = sb("scale_rows", [P, S], U8)
         first_pick = sb("first_pick", [P, S], U32)
-        nc.vector.tensor_copy(scale_pick[:], scale_tab[:].indirect(offs_sb[:]))
+        nc.vector.tensor_copy(scale_rows[:], scale_tab[:].indirect(offs_sb[:]))
+        for q in range(4):
+            nc.sync.dma_start(out=scale_pick[32 * q : 32 * q + 8, :].bitcast(I32), in_=scale_rows[32 * q + ROW0 : 32 * q + 32, :].bitcast(I32))
+        w_raw[0, 1] = sb("w1_raw1", [P, PACK * N], F32, tag="scale_tab")
+        load_weight(0, 1)
         nc.vector.tensor_copy(first_pick[:], word_tab[0][:].indirect(offs_sb[:]))
         second_pick = []
 
@@ -115,6 +118,9 @@ def tile_picked_edgeatt_tanh_p_kernel(tc, x_words, x_scales, w1, w2, w3, offs, s
             )
 
         interleave(w1_grp[0][:], 0, 0)
+        for i, z in ((1, 0), (1, 1), (2, 0), (2, 1)):
+            w_raw[i, z] = at("w%d_raw%d" % (i + 1, z), [P, PACK * N], F32, 2048 * (2 * i + z - 1))
+            load_weight(i, z)
         quantise(w1_grp[0][:], 0, 0, N)
         for a, b in Y_PIECES:
             product(0, 0, a, b)
@@ -133,7 +139,7 @@ def tile_picked_edgeatt_tanh_p_kernel(tc, x_words, x_scales, w1, w2, w3, offs, s
         for z in range(PASSES):
             interleave(w2_grp[:, z * K_PASS : (z + 1) * K_PASS], 1, z)
         quantise(w2_grp[:], 1, 0, 2 * N)
-        y = sb("y", [P, S], F32, tag="w_raw1")
+        y = at("y", [P, S], F32, 2048)
         for a, b in Y_PIECES[0::2]:
             nc.scalar.copy(out=y[:, a:b], in_=banks[0, a][:])
         for a, b in Y_PIECES[1::2]:

@@ -22,7 +22,7 @@ K_PASS = P * PACK
 PASSES = K // K_PASS
 GROUP = 16
 HALF = 512
-ROW0 = 24
+ROW0 = 96
 PICK_PIECES = ((512, 768), (768, 1024))
 Y_PIECES = ((0, 512), (512, 768), (768, 896), (896, 1024))
 HALVES = ((0, 512), (512, 1024))
@@ -49,7 +49,7 @@ def tile_picked_edgeatt_tanh_p_kernel(tc, x_words, x_scales, w1, w2, w3, offs, s
         src_sb = keep.tile([P, U // GROUP], U16, name="src_sb")
         dst_sb = keep.tile([P, U // GROUP], U16, name="dst_sb")
         scale_tab = sb("scale_tab", [P, T], U8)
-        scale_pick = sb("scale_pick", [P, S], U8)
+        scale_pick = sb("scale_pick", [P, PASSES * S], U8)
         word_tab = [at("word_tab0", [P, T], U32, 4096), sb("word_tab1", [P, T], U32)]
         w_raw = {(0, 0): at("w1_raw0", [P, PACK * N], F32, 512)}
         w_code = [sb("w_code%d" % i, [P, PASSES * N], U32) for i in range(3)]
@@ -66,9 +66,8 @@ def tile_picked_edgeatt_tanh_p_kernel(tc, x_words, x_scales, w1, w2, w3, offs, s
             nc.sync.dma_start(out=w_raw[i, z][:], in_=weights[i][z * K_PASS : (z + 1) * K_PASS, :].rearrange("(p j) m -> p (j m)", j=PACK))
 
         nc.sync.dma_start(offs_sb[:], offs)
-        for q in range(4):
-            nc.vector.memset(scale_tab[32 * q : 32 * q + ROW0, :].bitcast(I32), 0)
-            nc.sync.dma_start(out=scale_tab[32 * q + ROW0 : 32 * q + 32, :].bitcast(I32), in_=x_scales[:, 4 * q : 4 * q + 4, :].bitcast(I32))
+        nc.vector.memset(scale_tab[0:ROW0, :].bitcast(I32), 0)
+        nc.sync.dma_start(out=scale_tab[ROW0:P, :].bitcast(I32), in_=x_scales.rearrange("z r t -> r z t").bitcast(I32))
         load_words(0)
         load_weight(0, 0)
         nc.sync.dma_start(dst_sb[:], dst)
@@ -88,7 +87,7 @@ def tile_picked_edgeatt_tanh_p_kernel(tc, x_words, x_scales, w1, w2, w3, offs, s
         first_pick = sb("first_pick", [P, S], U32)
         nc.vector.tensor_copy(scale_rows[:], scale_tab[:].indirect(offs_sb[:]))
         for q in range(4):
-            nc.sync.dma_start(out=scale_pick[32 * q : 32 * q + 8, :].bitcast(I32), in_=scale_rows[32 * q + ROW0 : 32 * q + 32, :].bitcast(I32))
+            nc.sync.dma_start(out=scale_pick[32 * q : 32 * q + 4, :].bitcast(I32).rearrange("p (z s) -> p z s", z=PASSES), in_=scale_rows[ROW0 + 8 * q : ROW0 + 8 * q + 8, :].bitcast(I32))
         w_raw[0, 1] = sb("w1_raw1", [P, PACK * N], F32, tag="scale_tab")
         load_weight(0, 1)
         nc.vector.tensor_copy(first_pick[:], word_tab[0][:].indirect(offs_sb[:]))
@@ -112,7 +111,7 @@ def tile_picked_edgeatt_tanh_p_kernel(tc, x_words, x_scales, w1, w2, w3, offs, s
                 lhsT=w_code[i][:, z * N : (z + 1) * N].bitcast(FP8X4),
                 lhsT_scale=w_scale[i][:, z * N : (z + 1) * N],
                 rhs=picked(z, a, b).bitcast(FP8X4),
-                rhs_scale=scale_pick[4 * z :, a:b],
+                rhs_scale=scale_pick[:, z * S + a : z * S + b],
                 start=(z == 0),
                 stop=(z == PASSES - 1),
             )

@@ -23,7 +23,8 @@ PASSES = K // K_PASS
 GROUP = 16
 HALF = 512
 ROW0 = 96
-PICK_PIECES = ((512, 768), (768, 1024))
+PICK_CUT = 768
+GROUPS = ((0, 512), (512, 768), (768, 1024))
 Y_PIECES = ((0, 512), (512, 768), (768, 896), (896, 1024))
 HALVES = ((0, 512), (512, 1024))
 EDGE_PIECES = ((0, 512), (512, 896), (896, 1024))
@@ -48,10 +49,10 @@ def tile_picked_edgeatt_tanh_p_kernel(tc, x_words, x_scales, w1, w2, w3, offs, s
         offs_sb = keep.tile([P, S // GROUP], U16, name="offs_sb")
         src_sb = keep.tile([P, U // GROUP], U16, name="src_sb")
         dst_sb = keep.tile([P, U // GROUP], U16, name="dst_sb")
-        scale_tab = sb("scale_tab", [P, T], U8)
-        scale_pick = sb("scale_pick", [P, PASSES * S], U8)
-        word_tab = [at("word_tab0", [P, T], U32, 4096), sb("word_tab1", [P, T], U32)]
-        w_raw = {(0, 0): at("w1_raw0", [P, PACK * N], F32, 512)}
+        scale_tab = at("scale_tab", [P, T], U8, 3072)
+        scale_pick = sb("scale_pick", [P, S], U8)
+        word_tab = [at("word_tab0", [P, T], U32, 6144), sb("word_tab1", [P, T], U32)]
+        w_raw = {(0, z): sb("w1_raw%d" % z, [P, PACK * N], F32) for z in range(PASSES)}
         w_code = [sb("w_code%d" % i, [P, PASSES * N], U32) for i in range(3)]
         w_scale = [sb("w_scale%d" % i, [P, PASSES * N], U8) for i in range(3)]
         w1_grp = [sb("w1_grp%d" % z, [P, N * PACK], BF16) for z in range(PASSES)]
@@ -67,17 +68,19 @@ def tile_picked_edgeatt_tanh_p_kernel(tc, x_words, x_scales, w1, w2, w3, offs, s
 
         nc.sync.dma_start(offs_sb[:], offs)
         nc.vector.memset(scale_tab[0:ROW0, :].bitcast(I32), 0)
-        nc.sync.dma_start(out=scale_tab[ROW0:P, :].bitcast(I32), in_=x_scales.rearrange("z r t -> r z t").bitcast(I32))
+        for z in range(PASSES):
+            nc.sync.dma_start(out=scale_tab[ROW0 + 16 * z : ROW0 + 16 * z + 16, :].bitcast(I32), in_=x_scales[z].rearrange("(q i) t -> i q t", q=4).bitcast(I32))
         load_words(0)
         load_weight(0, 0)
         nc.sync.dma_start(dst_sb[:], dst)
         nc.sync.dma_start(src_sb[:], src)
         load_words(1)
+        load_weight(0, 1)
 
         def interleave(grouped, i, z):
             nc.scalar.copy(
                 out=grouped.rearrange("p (c i t) -> p c t i", i=4, t=PACK),
-                in_=w_raw[i, z][:].rearrange("p (t c i) -> p c t i", i=4, t=PACK),
+                in_=w_raw[i, z][:, :].rearrange("p (t c i) -> p c t i", i=4, t=PACK),
             )
 
         def quantise(grouped, i, a, b):
@@ -86,17 +89,21 @@ def tile_picked_edgeatt_tanh_p_kernel(tc, x_words, x_scales, w1, w2, w3, offs, s
         scale_rows = sb("scale_rows", [P, S], U8)
         first_pick = sb("first_pick", [P, S], U32)
         nc.vector.tensor_copy(scale_rows[:], scale_tab[:].indirect(offs_sb[:]))
-        for q in range(4):
-            nc.sync.dma_start(out=scale_pick[32 * q : 32 * q + 4, :].bitcast(I32).rearrange("p (z s) -> p z s", z=PASSES), in_=scale_rows[ROW0 + 8 * q : ROW0 + 8 * q + 8, :].bitcast(I32))
-        w_raw[0, 1] = sb("w1_raw1", [P, PACK * N], F32, tag="scale_tab")
-        load_weight(0, 1)
+        for q in (0, 2, 1, 3):
+            nc.sync.dma_start(out=scale_pick[32 * q : 32 * q + 8, :].bitcast(I32), in_=scale_rows[ROW0 + q : P : 4, :].bitcast(I32))
+        for z in range(PASSES):
+            w_raw[1, z] = at("w2_raw%d" % z, [P, PACK * N], F32, 2048 * (z + 1))
+            load_weight(1, z)
         nc.vector.tensor_copy(first_pick[:], word_tab[0][:].indirect(offs_sb[:]))
+        for z in range(PASSES):
+            w_raw[2, z] = at("w3_raw%d" % z, [P, PACK * N], F32, 2048 * (z + 3))
+            load_weight(2, z)
         second_pick = []
 
         def picked(z, a, b):
             if z == 0:
                 return first_pick[:, a:b]
-            return second_pick[a // HALF][:, a % HALF : a % HALF + b - a]
+            return second_pick[a // PICK_CUT][:, a % PICK_CUT : a % PICK_CUT + b - a]
 
         def pick_second(a, b):
             nc.vector.tensor_copy(picked(1, a, b), word_tab[1][:].indirect(entries(offs_sb, a, b)))
@@ -104,36 +111,31 @@ def tile_picked_edgeatt_tanh_p_kernel(tc, x_words, x_scales, w1, w2, w3, offs, s
         banks = {}
 
         def product(i, z, a, b):
-            if z == 0:
-                banks[i, a] = psum.tile([P, b - a], F32, name="acc%d_%d" % (i, a))
+            first = a if i == 0 else a // HALF * HALF
+            if (i, first) not in banks:
+                banks[i, first] = psum.tile([P, b - a if i == 0 else HALF], F32, name="acc%d_%d" % (i, first))
             nc.tensor.matmul_mx(
-                out=banks[i, a][:],
+                out=banks[i, first][:, a - first : b - first],
                 lhsT=w_code[i][:, z * N : (z + 1) * N].bitcast(FP8X4),
                 lhsT_scale=w_scale[i][:, z * N : (z + 1) * N],
                 rhs=picked(z, a, b).bitcast(FP8X4),
-                rhs_scale=scale_pick[:, z * S + a : z * S + b],
+                rhs_scale=scale_pick[4 * z :, a:b],
                 start=(z == 0),
                 stop=(z == PASSES - 1),
             )
 
         interleave(w1_grp[0][:], 0, 0)
-        for i, z in ((1, 0), (1, 1), (2, 0), (2, 1)):
-            w_raw[i, z] = at("w%d_raw%d" % (i + 1, z), [P, PACK * N], F32, 2048 * (2 * i + z - 1))
-            load_weight(i, z)
         quantise(w1_grp[0][:], 0, 0, N)
         for a, b in Y_PIECES:
             product(0, 0, a, b)
-        second_pick.append(sb("second_pick0", [P, HALF], U32))
-        pick_second(0, HALF)
+        second_pick.append(sb("second_pick0", [P, PICK_CUT], U32))
+        pick_second(0, PICK_CUT)
         interleave(w1_grp[1][:], 0, 1)
         quantise(w1_grp[1][:], 0, N, 2 * N)
-        product(0, 1, 0, HALF)
-        second_pick.append(sb("second_pick1", [P, HALF], U32, tag="w1_grp1"))
-        for a, b in PICK_PIECES:
-            pick_second(a, b)
-            for c, d in Y_PIECES:
-                if a <= c < b:
-                    product(0, 1, c, d)
+        second_pick.append(sb("second_pick1", [P, S - PICK_CUT], U32, tag="w1_grp1"))
+        pick_second(PICK_CUT, S)
+        for a, b in Y_PIECES:
+            product(0, 1, a, b)
 
         for z in range(PASSES):
             interleave(w2_grp[:, z * K_PASS : (z + 1) * K_PASS], 1, z)
@@ -143,7 +145,7 @@ def tile_picked_edgeatt_tanh_p_kernel(tc, x_words, x_scales, w1, w2, w3, offs, s
             nc.scalar.copy(out=y[:, a:b], in_=banks[0, a][:])
         for a, b in Y_PIECES[1::2]:
             nc.vector.tensor_copy(out=y[:, a:b], in_=banks[0, a][:])
-        for a, b in HALVES:
+        for a, b in GROUPS:
             for z in range(PASSES):
                 product(1, z, a, b)
 
@@ -159,9 +161,10 @@ def tile_picked_edgeatt_tanh_p_kernel(tc, x_words, x_scales, w1, w2, w3, offs, s
         h = sb("h", [P, S], F32)
         for a, b in HALVES:
             nc.scalar.copy(out=e[:, a:b], in_=banks[1, a][:])
-        for a, b in HALVES:
+        for a, b in GROUPS:
             for z in range(PASSES):
                 product(2, z, a, b)
+        for a, b in HALVES:
             nc.scalar.copy(out=h[:, a:b], in_=banks[2, a][:])
 
         pre = sb("pre", [P, U], F32)

@@ -72,8 +72,6 @@ def tile_picked_edgeatt_tanh_p_kernel(tc, x_words, x_scales, w1, w2, w3, offs, s
             nc.sync.dma_start(out=scale_tab[ROW0 + 16 * z : ROW0 + 16 * z + 16, :].bitcast(I32), in_=x_scales[z].rearrange("(q i) t -> i q t", q=4).bitcast(I32))
         load_words(0)
         load_weight(0, 0)
-        nc.sync.dma_start(dst_sb[:], dst)
-        nc.sync.dma_start(src_sb[:], src)
         load_words(1)
         load_weight(0, 1)
 
@@ -94,10 +92,12 @@ def tile_picked_edgeatt_tanh_p_kernel(tc, x_words, x_scales, w1, w2, w3, offs, s
         for z in range(PASSES):
             w_raw[1, z] = at("w2_raw%d" % z, [P, PACK * N], F32, 2048 * (z + 1))
             load_weight(1, z)
+        nc.sync.dma_start(dst_sb[:], dst)
         nc.vector.tensor_copy(first_pick[:], word_tab[0][:].indirect(offs_sb[:]))
         for z in range(PASSES):
             w_raw[2, z] = at("w3_raw%d" % z, [P, PACK * N], F32, 2048 * (z + 3))
             load_weight(2, z)
+        nc.sync.dma_start(src_sb[:], src)
         second_pick = []
 
         def picked(z, a, b):

@@ -124,6 +124,9 @@ def tile_picked_edgeatt_tanh_p_kernel(tc, x_words, x_scales, w1, w2, w3, offs, s
                 stop=(z == PASSES - 1),
             )
 
+        warm = psum.tile([P, HALF], F32, name="acc2_512")
+        for a, b in HALVES:
+            nc.tensor.matmul_mx(out=warm[:], lhsT=first_pick[:, 0:N].bitcast(FP8X4), lhsT_scale=scale_rows[:, 0:N], rhs=first_pick[:, a:b].bitcast(FP8X4), rhs_scale=scale_rows[:, a:b], start=True, stop=True)
         interleave(w1_grp[0][:], 0, 0)
         quantise(w1_grp[0][:], 0, 0, N)
         for a, b in Y_PIECES:

@@ -135,7 +135,7 @@ def tile_picked_edgeatt_tanh_p_kernel(tc, x_words, x_scales, w1, w2, w3, offs, s
         pick_second(0, PICK_CUT)
         interleave(w1_grp[1][:], 0, 1)
         quantise(w1_grp[1][:], 0, N, 2 * N)
-        second_pick.append(sb("second_pick1", [P, S - PICK_CUT], U32, tag="w1_grp1"))
+        second_pick.append(sb("second_pick1", [P, S - PICK_CUT], U32, tag="w1_raw1"))
         pick_second(PICK_CUT, S)
         for a, b in Y_PIECES:
             product(0, 1, a, b)
@@ -157,7 +157,7 @@ def tile_picked_edgeatt_tanh_p_kernel(tc, x_words, x_scales, w1, w2, w3, offs, s
         for z in range(PASSES):
             interleave(w3_grp[:, z * K_PASS : (z + 1) * K_PASS], 2, z)
         quantise(w3_grp[:], 2, 0, 2 * N)
-        y_dst.append(sb("y_dst1", [P, HALF], F32, tag="w3_grp"))
+        y_dst.append(at("y_dst1", [P, HALF], F32, 8192))
         nc.vector.tensor_copy(y_dst[1][:], y[:].indirect(entries(dst_sb, HALF, U)))
 
         e = sb("e", [P, S], F32)

@@ -66,10 +66,10 @@ def tile_picked_edgeatt_tanh_p_kernel(tc, x_words, x_scales, w1, w2, w3, offs, s
         def load_weight(i, z):
             nc.sync.dma_start(out=w_raw[i, z][:], in_=weights[i][z * K_PASS : (z + 1) * K_PASS, :].rearrange("(p j) m -> p (j m)", j=PACK))
 
-        nc.sync.dma_start(offs_sb[:], offs)
         nc.vector.memset(scale_tab[0:ROW0, :].bitcast(I32), 0)
         for z in range(PASSES):
             nc.sync.dma_start(out=scale_tab[ROW0 + 16 * z : ROW0 + 16 * z + 16, :].bitcast(I32), in_=x_scales[z].rearrange("(q i) t -> i q t", q=4).bitcast(I32))
+        nc.sync.dma_start(offs_sb[:], offs)
         load_words(0)
         load_weight(0, 0)
         load_words(1)

@@ -22,7 +22,7 @@ K_PASS = P * PACK
 PASSES = K // K_PASS
 GROUP = 16
 HALF = 512
-ROW0 = 96
+QUAD = 32
 PICK_CUT = 768
 GROUPS = ((0, 512), (512, 768), (768, 1024))
 Y_PIECES = ((0, 512), (512, 768), (768, 896), (896, 1024))
@@ -66,9 +66,10 @@ def tile_picked_edgeatt_tanh_p_kernel(tc, x_words, x_scales, w1, w2, w3, offs, s
         def load_weight(i, z):
             nc.sync.dma_start(out=w_raw[i, z][:], in_=weights[i][z * K_PASS : (z + 1) * K_PASS, :].rearrange("(p j) m -> p (j m)", j=PACK))
 
-        nc.vector.memset(scale_tab[0:ROW0, :].bitcast(I32), 0)
-        for z in range(PASSES):
-            nc.sync.dma_start(out=scale_tab[ROW0 + 16 * z : ROW0 + 16 * z + 16, :].bitcast(I32), in_=x_scales[z].rearrange("(q i) t -> i q t", q=4).bitcast(I32))
+        nc.vector.memset(scale_tab[QUAD : 2 * QUAD, :].bitcast(I32), 0)
+        nc.vector.memset(scale_tab[2 * QUAD : P, :].bitcast(I32), 0)
+        for z in reversed(range(PASSES)):
+            nc.sync.dma_start(out=scale_tab[16 * z : 16 * z + 16, :].bitcast(I32), in_=x_scales[z].rearrange("(q i) t -> i q t", q=4).bitcast(I32))
         nc.sync.dma_start(offs_sb[:], offs)
         load_words(0)
         load_weight(0, 0)
@@ -88,7 +89,7 @@ def tile_picked_edgeatt_tanh_p_kernel(tc, x_words, x_scales, w1, w2, w3, offs, s
         first_pick = sb("first_pick", [P, S], U32)
         nc.vector.tensor_copy(scale_rows[:], scale_tab[:].indirect(offs_sb[:]))
         for q in (0, 2, 1, 3):
-            nc.sync.dma_start(out=scale_pick[32 * q : 32 * q + 8, :].bitcast(I32), in_=scale_rows[ROW0 + q : P : 4, :].bitcast(I32))
+            nc.sync.dma_start(out=scale_pick[32 * q : 32 * q + 8, :].bitcast(I32), in_=scale_rows[q:QUAD:4, :].bitcast(I32))
         for z in range(PASSES):
             w_raw[1, z] = at("w2_raw%d" % z, [P, PACK * N], F32, 2048 * (z + 1))
             load_weight(1, z)

@@ -15,6 +15,7 @@ FP8X4 = mybir.dt.float8_e4m3fn_x4
 ADD = mybir.AluOpType.add
 MULT = mybir.AluOpType.mult
 TANH = mybir.ActivationFunctionType.Tanh
+COPY = mybir.ActivationFunctionType.Copy
 
 P = 128
 PACK = 4
@@ -24,10 +25,10 @@ GROUP = 16
 HALF = 512
 QUAD = 32
 PICK_CUT = 768
-GROUPS = ((0, 512), (512, 768), (768, 1024))
-Y_PIECES = ((0, 512), (512, 768), (768, 896), (896, 1024))
+Y_PIECES = ((0, 512), (512, 768), (768, 1024))
 HALVES = ((0, 512), (512, 1024))
-EDGE_PIECES = ((0, 512), (512, 896), (896, 1024))
+FUSED = 640
+EDGE_PIECES = ((0, 512), (512, 640), (640, 896), (896, 1024))
 
 
 def tile_picked_edgeatt_tanh_p_kernel(tc, x_words, x_scales, w1, w2, w3, offs, src, dst, out):
@@ -46,58 +47,57 @@ def tile_picked_edgeatt_tanh_p_kernel(tc, x_words, x_scales, w1, w2, w3, offs, s
         def entries(lst, a, b):
             return lst[:, a // GROUP : b // GROUP]
 
+        def rows(w, z):
+            return w[z * K_PASS : (z + 1) * K_PASS, :].rearrange("(p j) m -> p (j m)", j=PACK)
+
         offs_sb = keep.tile([P, S // GROUP], U16, name="offs_sb")
         src_sb = keep.tile([P, U // GROUP], U16, name="src_sb")
         dst_sb = keep.tile([P, U // GROUP], U16, name="dst_sb")
         scale_tab = at("scale_tab", [P, T], U8, 3072)
+        scale_rows = sb("scale_rows", [P, S], U8)
         scale_pick = sb("scale_pick", [P, S], U8)
         word_tab = [at("word_tab0", [P, T], U32, 6144), sb("word_tab1", [P, T], U32)]
-        w_raw = {(0, z): sb("w1_raw%d" % z, [P, PACK * N], F32) for z in range(PASSES)}
+        w1_raw = [sb("w1_raw%d" % z, [P, K_PASS], F32) for z in range(PASSES)]
+        w_grp = [sb("w_grp%d" % i, [P, PASSES * K_PASS], BF16) for i in range(3)]
         w_code = [sb("w_code%d" % i, [P, PASSES * N], U32) for i in range(3)]
         w_scale = [sb("w_scale%d" % i, [P, PASSES * N], U8) for i in range(3)]
-        w1_grp = [sb("w1_grp%d" % z, [P, N * PACK], BF16) for z in range(PASSES)]
-        w2_grp = sb("w2_grp", [P, PASSES * N * PACK], BF16)
-        w3_grp = sb("w3_grp", [P, PASSES * N * PACK], BF16)
-        weights = (w1, w2, w3)
 
         def load_words(z):
             nc.sync.dma_start(out=word_tab[z][:].bitcast(I32), in_=x_words[z].rearrange("p n t -> p (n t)").bitcast(I32))
-
-        def load_weight(i, z):
-            nc.sync.dma_start(out=w_raw[i, z][:], in_=weights[i][z * K_PASS : (z + 1) * K_PASS, :].rearrange("(p j) m -> p (j m)", j=PACK))
 
         nc.vector.memset(scale_tab[QUAD : 2 * QUAD, :].bitcast(I32), 0)
         nc.vector.memset(scale_tab[2 * QUAD : P, :].bitcast(I32), 0)
         for z in reversed(range(PASSES)):
             nc.sync.dma_start(out=scale_tab[16 * z : 16 * z + 16, :].bitcast(I32), in_=x_scales[z].rearrange("(q i) t -> i q t", q=4).bitcast(I32))
         nc.sync.dma_start(offs_sb[:], offs)
-        load_words(0)
-        load_weight(0, 0)
-        load_words(1)
-        load_weight(0, 1)
+        for z in range(PASSES):
+            load_words(z)
+            nc.sync.dma_start(out=w1_raw[z][:], in_=rows(w1, z))
 
-        def interleave(grouped, i, z):
+        def grouped(i, z0, z1):
+            return w_grp[i][:, z0 * K_PASS : z1 * K_PASS]
+
+        def round_on_scalar(i, z, raw):
             nc.scalar.copy(
-                out=grouped.rearrange("p (c i t) -> p c t i", i=4, t=PACK),
-                in_=w_raw[i, z][:, :].rearrange("p (t c i) -> p c t i", i=4, t=PACK),
+                out=grouped(i, z, z + 1).rearrange("p (c i t) -> p c t i", i=4, t=PACK),
+                in_=raw.rearrange("p (t c i) -> p c t i", i=4, t=PACK),
             )
 
-        def quantise(grouped, i, a, b):
-            nc.vector.quantize_mx(out=w_code[i][:, a:b].bitcast(FP8X4), scales=w_scale[i][:, a:b], in_=grouped)
+        def quantise(i, z0, z1):
+            nc.vector.quantize_mx(out=w_code[i][:, z0 * N : z1 * N].bitcast(FP8X4), scales=w_scale[i][:, z0 * N : z1 * N], in_=grouped(i, z0, z1))
 
-        scale_rows = sb("scale_rows", [P, S], U8)
-        first_pick = sb("first_pick", [P, S], U32)
         nc.vector.tensor_copy(scale_rows[:], scale_tab[:].indirect(offs_sb[:]))
         for q in (0, 2, 1, 3):
             nc.sync.dma_start(out=scale_pick[32 * q : 32 * q + 8, :].bitcast(I32), in_=scale_rows[q:QUAD:4, :].bitcast(I32))
+        w2_raw = [at("w2_raw%d" % z, [P, K_PASS], F32, 2048 * (z + 1)) for z in range(PASSES)]
         for z in range(PASSES):
-            w_raw[1, z] = at("w2_raw%d" % z, [P, PACK * N], F32, 2048 * (z + 1))
-            load_weight(1, z)
+            nc.sync.dma_start(out=w2_raw[z][:], in_=rows(w2, z))
         nc.sync.dma_start(dst_sb[:], dst)
+        first_pick = sb("first_pick", [P, S], U32)
         nc.vector.tensor_copy(first_pick[:], word_tab[0][:].indirect(offs_sb[:]))
+        w3_raw = at("w3_raw", [P, PASSES * K_PASS], F32, 6144)
         for z in range(PASSES):
-            w_raw[2, z] = at("w3_raw%d" % z, [P, PACK * N], F32, 2048 * (z + 3))
-            load_weight(2, z)
+            nc.sync.dma_start(out=w3_raw[:, z * K_PASS : (z + 1) * K_PASS], in_=rows(w3, z))
         nc.sync.dma_start(src_sb[:], src)
         second_pick = []
 
@@ -125,58 +125,61 @@ def tile_picked_edgeatt_tanh_p_kernel(tc, x_words, x_scales, w1, w2, w3, offs, s
                 stop=(z == PASSES - 1),
             )
 
-        warm = psum.tile([P, HALF], F32, name="acc2_512")
-        for a, b in HALVES:
-            nc.tensor.matmul_mx(out=warm[:], lhsT=first_pick[:, 0:N].bitcast(FP8X4), lhsT_scale=scale_rows[:, 0:N], rhs=first_pick[:, a:b].bitcast(FP8X4), rhs_scale=scale_rows[:, a:b], start=True, stop=True)
-        interleave(w1_grp[0][:], 0, 0)
-        quantise(w1_grp[0][:], 0, 0, N)
+        round_on_scalar(0, 0, w1_raw[0][:])
+        quantise(0, 0, 1)
         for a, b in Y_PIECES:
             product(0, 0, a, b)
         second_pick.append(sb("second_pick0", [P, PICK_CUT], U32))
         pick_second(0, PICK_CUT)
-        interleave(w1_grp[1][:], 0, 1)
-        quantise(w1_grp[1][:], 0, N, 2 * N)
+        round_on_scalar(0, 1, w1_raw[1][:])
+        quantise(0, 1, 2)
         second_pick.append(sb("second_pick1", [P, S - PICK_CUT], U32, tag="w1_raw1"))
         pick_second(PICK_CUT, S)
         for a, b in Y_PIECES:
             product(0, 1, a, b)
 
         for z in range(PASSES):
-            interleave(w2_grp[:, z * K_PASS : (z + 1) * K_PASS], 1, z)
-        quantise(w2_grp[:], 1, 0, 2 * N)
+            round_on_scalar(1, z, w2_raw[z][:])
+        quantise(1, 0, 2)
         y = at("y", [P, S], F32, 2048)
-        for a, b in Y_PIECES[0::2]:
+        for a, b in Y_PIECES[:2]:
             nc.scalar.copy(out=y[:, a:b], in_=banks[0, a][:])
-        for a, b in Y_PIECES[1::2]:
+        for a, b in Y_PIECES[2:]:
             nc.vector.tensor_copy(out=y[:, a:b], in_=banks[0, a][:])
-        for a, b in GROUPS:
+        for a, b in Y_PIECES:
             for z in range(PASSES):
                 product(1, z, a, b)
 
-        y_dst = [sb("y_dst0", [P, HALF], F32, tag="w2_grp")]
-        nc.vector.tensor_copy(y_dst[0][:], y[:].indirect(entries(dst_sb, 0, HALF)))
-        for z in range(PASSES):
-            interleave(w3_grp[:, z * K_PASS : (z + 1) * K_PASS], 2, z)
-        quantise(w3_grp[:], 2, 0, 2 * N)
-        y_dst.append(at("y_dst1", [P, HALF], F32, 8192))
-        nc.vector.tensor_copy(y_dst[1][:], y[:].indirect(entries(dst_sb, HALF, U)))
+        y_dst = sb("y_dst", [P, U], F32)
+        for a, b in HALVES:
+            nc.scalar.activation(y_dst[:, a:b], y[:].indirect(entries(dst_sb, a, b)), COPY)
 
+        nc.vector.tensor_copy(
+            out=w_grp[2][:].rearrange("p (z c i t) -> p z c t i", z=PASSES, i=4, t=PACK),
+            in_=w3_raw[:].rearrange("p (z t c i) -> p z c t i", z=PASSES, i=4, t=PACK),
+        )
         e = sb("e", [P, S], F32)
         h = sb("h", [P, S], F32)
         for a, b in HALVES:
-            nc.scalar.copy(out=e[:, a:b], in_=banks[1, a][:])
-        for a, b in GROUPS:
+            nc.vector.tensor_copy(out=e[:, a:b], in_=banks[1, a][:])
+        quantise(2, 0, 2)
+        for a, b in Y_PIECES:
             for z in range(PASSES):
                 product(2, z, a, b)
-        for a, b in HALVES:
-            nc.scalar.copy(out=h[:, a:b], in_=banks[2, a][:])
 
         pre = sb("pre", [P, U], F32)
         gate = sb("gate", [P, U], F32, tag="scale_pick")
         msg = sb("msg", [P, U], F32)
         for a, b in HALVES:
-            nc.vector.tensor_tensor(pre[:, a:b], e[:].indirect(entries(src_sb, a, b)), y_dst[a // HALF][:], ADD)
+            nc.vector.tensor_tensor(pre[:, a:b], e[:].indirect(entries(src_sb, a, b)), y_dst[:, a:b], ADD)
+            nc.scalar.copy(out=h[:, a:b], in_=banks[2, a][:])
+        for a, b in HALVES:
             nc.scalar.activation(gate[:, a:b], pre[:, a:b], TANH)
+        h_src = sb("h_src", [P, U - FUSED], F32)
+        nc.scalar.activation(h_src[:], h[:].indirect(entries(src_sb, FUSED, U)), COPY)
         for a, b in EDGE_PIECES:
-            nc.vector.tensor_tensor(msg[:, a:b], h[:].indirect(entries(src_sb, a, b)), gate[:, a:b], MULT)
+            if b <= FUSED:
+                nc.vector.tensor_tensor(msg[:, a:b], h[:].indirect(entries(src_sb, a, b)), gate[:, a:b], MULT)
+            else:
+                nc.vector.tensor_tensor(msg[:, a:b], h_src[:, a - FUSED : b - FUSED], gate[:, a:b], MULT)
             nc.sync.dma_start(out=out[:, a:b], in_=msg[:, a:b])

@@ -24,11 +24,13 @@ PASSES = K // K_PASS
 GROUP = 16
 HALF = 512
 QUAD = 32
-PICK_CUT = 768
-Y_PIECES = ((0, 512), (512, 768), (768, 1024))
+PICK_CUT = 640
+LAST_CUT = 896
+PIECES = ((0, 512), (512, 640), (640, 896), (896, 1024))
+Y_BANKS = ((0, 512), (512, 640), (640, 1024))
 HALVES = ((0, 512), (512, 1024))
 FUSED = 640
-EDGE_PIECES = ((0, 512), (512, 640), (640, 896), (896, 1024))
+EDGE_PIECES = ((0, 256), (256, 512), (512, 640), (640, 896), (896, 1024))
 
 
 def tile_picked_edgeatt_tanh_p_kernel(tc, x_words, x_scales, w1, w2, w3, offs, src, dst, out):
@@ -70,9 +72,9 @@ def tile_picked_edgeatt_tanh_p_kernel(tc, x_words, x_scales, w1, w2, w3, offs, s
         for z in reversed(range(PASSES)):
             nc.sync.dma_start(out=scale_tab[16 * z : 16 * z + 16, :].bitcast(I32), in_=x_scales[z].rearrange("(q i) t -> i q t", q=4).bitcast(I32))
         nc.sync.dma_start(offs_sb[:], offs)
-        for z in range(PASSES):
-            load_words(z)
-            nc.sync.dma_start(out=w1_raw[z][:], in_=rows(w1, z))
+        load_words(0)
+        nc.sync.dma_start(out=w1_raw[0][:], in_=rows(w1, 0))
+        load_words(1)
 
         def grouped(i, z0, z1):
             return w_grp[i][:, z0 * K_PASS : z1 * K_PASS]
@@ -89,22 +91,25 @@ def tile_picked_edgeatt_tanh_p_kernel(tc, x_words, x_scales, w1, w2, w3, offs, s
         nc.vector.tensor_copy(scale_rows[:], scale_tab[:].indirect(offs_sb[:]))
         for q in (0, 2, 1, 3):
             nc.sync.dma_start(out=scale_pick[32 * q : 32 * q + 8, :].bitcast(I32), in_=scale_rows[q:QUAD:4, :].bitcast(I32))
+        nc.sync.dma_start(out=w1_raw[1][:], in_=rows(w1, 1))
         w2_raw = [at("w2_raw%d" % z, [P, K_PASS], F32, 2048 * (z + 1)) for z in range(PASSES)]
         for z in range(PASSES):
             nc.sync.dma_start(out=w2_raw[z][:], in_=rows(w2, z))
-        nc.sync.dma_start(dst_sb[:], dst)
         first_pick = sb("first_pick", [P, S], U32)
         nc.vector.tensor_copy(first_pick[:], word_tab[0][:].indirect(offs_sb[:]))
         w3_raw = at("w3_raw", [P, PASSES * K_PASS], F32, 6144)
-        for z in range(PASSES):
-            nc.sync.dma_start(out=w3_raw[:, z * K_PASS : (z + 1) * K_PASS], in_=rows(w3, z))
+        nc.sync.dma_start(out=w3_raw[:, :K_PASS], in_=rows(w3, 0))
+        nc.sync.dma_start(dst_sb[:], dst)
+        nc.sync.dma_start(out=w3_raw[:, K_PASS:], in_=rows(w3, 1))
         nc.sync.dma_start(src_sb[:], src)
         second_pick = []
 
         def picked(z, a, b):
             if z == 0:
                 return first_pick[:, a:b]
-            return second_pick[a // PICK_CUT][:, a % PICK_CUT : a % PICK_CUT + b - a]
+            if a < PICK_CUT:
+                return second_pick[0][:, a:b]
+            return second_pick[1][:, a - PICK_CUT : b - PICK_CUT]
 
         def pick_second(a, b):
             nc.vector.tensor_copy(picked(1, a, b), word_tab[1][:].indirect(entries(offs_sb, a, b)))
@@ -112,43 +117,49 @@ def tile_picked_edgeatt_tanh_p_kernel(tc, x_words, x_scales, w1, w2, w3, offs, s
         banks = {}
 
         def product(i, z, a, b):
-            first = a if i == 0 else a // HALF * HALF
+            first, last = [(u, v) for u, v in (Y_BANKS if i == 0 else HALVES) if u <= a < v][0]
             if (i, first) not in banks:
-                banks[i, first] = psum.tile([P, b - a if i == 0 else HALF], F32, name="acc%d_%d" % (i, first))
+                banks[i, first] = psum.tile([P, last - first], F32, name="acc%d_%d" % (i, first))
             nc.tensor.matmul_mx(
                 out=banks[i, first][:, a - first : b - first],
                 lhsT=w_code[i][:, z * N : (z + 1) * N].bitcast(FP8X4),
                 lhsT_scale=w_scale[i][:, z * N : (z + 1) * N],
                 rhs=picked(z, a, b).bitcast(FP8X4),
                 rhs_scale=scale_pick[4 * z :, a:b],
-                start=(z == 0),
-                stop=(z == PASSES - 1),
+                start=(z == 0 and a == first),
+                stop=(z == PASSES - 1 and b == last),
             )
+
+        def whole_product(i):
+            for first, last in HALVES:
+                product(i, 0, first, last)
+                for a, b in PIECES:
+                    if first <= a < last:
+                        product(i, 1, a, b)
 
         round_on_scalar(0, 0, w1_raw[0][:])
         quantise(0, 0, 1)
-        for a, b in Y_PIECES:
+        for a, b in PIECES:
             product(0, 0, a, b)
         second_pick.append(sb("second_pick0", [P, PICK_CUT], U32))
         pick_second(0, PICK_CUT)
         round_on_scalar(0, 1, w1_raw[1][:])
         quantise(0, 1, 2)
         second_pick.append(sb("second_pick1", [P, S - PICK_CUT], U32, tag="w1_raw1"))
-        pick_second(PICK_CUT, S)
-        for a, b in Y_PIECES:
+        pick_second(PICK_CUT, LAST_CUT)
+        pick_second(LAST_CUT, S)
+        for a, b in PIECES:
             product(0, 1, a, b)
 
         for z in range(PASSES):
             round_on_scalar(1, z, w2_raw[z][:])
         quantise(1, 0, 2)
         y = at("y", [P, S], F32, 2048)
-        for a, b in Y_PIECES[:2]:
+        for a, b in Y_BANKS[:2]:
             nc.scalar.copy(out=y[:, a:b], in_=banks[0, a][:])
-        for a, b in Y_PIECES[2:]:
+        for a, b in Y_BANKS[2:]:
             nc.vector.tensor_copy(out=y[:, a:b], in_=banks[0, a][:])
-        for a, b in Y_PIECES:
-            for z in range(PASSES):
-                product(1, z, a, b)
+        whole_product(1)
 
         y_dst = sb("y_dst", [P, U], F32)
         for a, b in HALVES:
@@ -160,12 +171,14 @@ def tile_picked_edgeatt_tanh_p_kernel(tc, x_words, x_scales, w1, w2, w3, offs, s
         )
         e = sb("e", [P, S], F32)
         h = sb("h", [P, S], F32)
+        nc.vector.tensor_copy(out=e[:, :HALF], in_=banks[1, 0][:])
+        quantise(2, 0, 1)
+        nc.vector.tensor_copy(out=e[:, HALF:], in_=banks[1, HALF][:])
+        quantise(2, 1, 2)
         for a, b in HALVES:
-            nc.vector.tensor_copy(out=e[:, a:b], in_=banks[1, a][:])
-        quantise(2, 0, 2)
-        for a, b in Y_PIECES:
-            for z in range(PASSES):
-                product(2, z, a, b)
+            product(2, 0, a, b)
+        for a, b in PIECES:
+            product(2, 1, a, b)
 
         pre = sb("pre", [P, U], F32)
         gate = sb("gate", [P, U], F32, tag="scale_pick")
@@ -173,13 +186,14 @@ def tile_picked_edgeatt_tanh_p_kernel(tc, x_words, x_scales, w1, w2, w3, offs, s
         for a, b in HALVES:
             nc.vector.tensor_tensor(pre[:, a:b], e[:].indirect(entries(src_sb, a, b)), y_dst[:, a:b], ADD)
             nc.scalar.copy(out=h[:, a:b], in_=banks[2, a][:])
-        for a, b in HALVES:
-            nc.scalar.activation(gate[:, a:b], pre[:, a:b], TANH)
-        h_src = sb("h_src", [P, U - FUSED], F32)
-        nc.scalar.activation(h_src[:], h[:].indirect(entries(src_sb, FUSED, U)), COPY)
+        h_src = {FUSED: sb("h_src0", [P, LAST_CUT - FUSED], F32), LAST_CUT: sb("h_src1", [P, U - LAST_CUT], F32, tag="y_dst")}
+        nc.scalar.activation(gate[:, :HALF], pre[:, :HALF], TANH)
+        nc.scalar.activation(h_src[FUSED][:], h[:].indirect(entries(src_sb, FUSED, LAST_CUT)), COPY)
+        nc.scalar.activation(gate[:, HALF:], pre[:, HALF:], TANH)
+        nc.scalar.activation(h_src[LAST_CUT][:], h[:].indirect(entries(src_sb, LAST_CUT, U)), COPY)
         for a, b in EDGE_PIECES:
             if b <= FUSED:
                 nc.vector.tensor_tensor(msg[:, a:b], h[:].indirect(entries(src_sb, a, b)), gate[:, a:b], MULT)
             else:
-                nc.vector.tensor_tensor(msg[:, a:b], h_src[:, a - FUSED : b - FUSED], gate[:, a:b], MULT)
+                nc.vector.tensor_tensor(msg[:, a:b], h_src[a][:], gate[:, a:b], MULT)
             nc.sync.dma_start(out=out[:, a:b], in_=msg[:, a:b])

@@ -27,7 +27,7 @@ QUAD = 32
 PICK_CUT = 640
 LAST_CUT = 896
 PIECES = ((0, 512), (512, 640), (640, 896), (896, 1024))
-Y_BANKS = ((0, 512), (512, 640), (640, 1024))
+Y_BANKS = ((0, 512), (512, 896), (896, 1024))
 HALVES = ((0, 512), (512, 1024))
 FUSED = 640
 EDGE_PIECES = ((0, 256), (256, 512), (512, 640), (640, 896), (896, 1024))

@@ -29,8 +29,9 @@ LAST_CUT = 896
 PIECES = ((0, 512), (512, 640), (640, 896), (896, 1024))
 Y_BANKS = ((0, 512), (512, 896), (896, 1024))
 HALVES = ((0, 512), (512, 1024))
-FUSED = 640
-EDGE_PIECES = ((0, 256), (256, 512), (512, 640), (640, 896), (896, 1024))
+PLAIN = ((512, 768), (896, 1024))
+EDGE_PIECES = ((0, 256), (256, 512), (512, 768), (768, 896), (896, 1024))
+TANH_PIECES = ((0, 256), (256, 512), (512, 768), (768, 1024))
 
 
 def tile_picked_edgeatt_tanh_p_kernel(tc, x_words, x_scales, w1, w2, w3, offs, src, dst, out):
@@ -186,13 +187,14 @@ def tile_picked_edgeatt_tanh_p_kernel(tc, x_words, x_scales, w1, w2, w3, offs, s
         for a, b in HALVES:
             nc.vector.tensor_tensor(pre[:, a:b], e[:].indirect(entries(src_sb, a, b)), y_dst[:, a:b], ADD)
             nc.scalar.copy(out=h[:, a:b], in_=banks[2, a][:])
-        h_src = {FUSED: sb("h_src0", [P, LAST_CUT - FUSED], F32), LAST_CUT: sb("h_src1", [P, U - LAST_CUT], F32, tag="y_dst")}
-        nc.scalar.activation(gate[:, :HALF], pre[:, :HALF], TANH)
-        nc.scalar.activation(h_src[FUSED][:], h[:].indirect(entries(src_sb, FUSED, LAST_CUT)), COPY)
-        nc.scalar.activation(gate[:, HALF:], pre[:, HALF:], TANH)
-        nc.scalar.activation(h_src[LAST_CUT][:], h[:].indirect(entries(src_sb, LAST_CUT, U)), COPY)
+        h_src = {}
+        for j, (first, last) in enumerate(PLAIN):
+            for a, b in TANH_PIECES[2 * j : 2 * j + 2]:
+                nc.scalar.activation(gate[:, a:b], pre[:, a:b], TANH)
+            h_src[first] = sb("h_src%d" % j, [P, last - first], F32, tag="y_dst" if j else None)
+            nc.scalar.activation(h_src[first][:], h[:].indirect(entries(src_sb, first, last)), COPY)
         for a, b in EDGE_PIECES:
-            if b <= FUSED:
+            if a not in h_src:
                 nc.vector.tensor_tensor(msg[:, a:b], h[:].indirect(entries(src_sb, a, b)), gate[:, a:b], MULT)
             else:
                 nc.vector.tensor_tensor(msg[:, a:b], h_src[a][:], gate[:, a:b], MULT)

@@ -24,10 +24,13 @@ PASSES = K // K_PASS
 GROUP = 16
 HALF = 512
 QUAD = 32
+W3_SCALAR = 8
 PICK_CUT = 640
 LAST_CUT = 896
 PIECES = ((0, 512), (512, 640), (640, 896), (896, 1024))
-Y_BANKS = ((0, 512), (512, 896), (896, 1024))
+Y_BANKS = ((0, 512), (512, 768), (768, 1024))
+H_BANKS = ((0, 512), (512, 896), (896, 1024))
+Y_PIECES = ((0, 512), (512, 640), (640, 768), (768, 896), (896, 1024))
 HALVES = ((0, 512), (512, 1024))
 PLAIN = ((512, 768), (896, 1024))
 EDGE_PIECES = ((0, 256), (256, 512), (512, 768), (768, 896), (896, 1024))
@@ -61,7 +64,7 @@ def tile_picked_edgeatt_tanh_p_kernel(tc, x_words, x_scales, w1, w2, w3, offs, s
         scale_pick = sb("scale_pick", [P, S], U8)
         word_tab = [at("word_tab0", [P, T], U32, 6144), sb("word_tab1", [P, T], U32)]
         w1_raw = [sb("w1_raw%d" % z, [P, K_PASS], F32) for z in range(PASSES)]
-        w_grp = [sb("w_grp%d" % i, [P, PASSES * K_PASS], BF16) for i in range(3)]
+        w_grp = [sb("w_grp%d" % i, [P, PASSES * K_PASS], BF16) for i in range(2)]
         w_code = [sb("w_code%d" % i, [P, PASSES * N], U32) for i in range(3)]
         w_scale = [sb("w_scale%d" % i, [P, PASSES * N], U8) for i in range(3)]
 
@@ -98,10 +101,10 @@ def tile_picked_edgeatt_tanh_p_kernel(tc, x_words, x_scales, w1, w2, w3, offs, s
             nc.sync.dma_start(out=w2_raw[z][:], in_=rows(w2, z))
         first_pick = sb("first_pick", [P, S], U32)
         nc.vector.tensor_copy(first_pick[:], word_tab[0][:].indirect(offs_sb[:]))
-        w3_raw = at("w3_raw", [P, PASSES * K_PASS], F32, 6144)
-        nc.sync.dma_start(out=w3_raw[:, :K_PASS], in_=rows(w3, 0))
+        w3_raw = at("w3_raw", [P, PASSES * K_PASS], F32, 8192)
+        for z in range(PASSES):
+            nc.sync.dma_start(out=w3_raw[:, z * K_PASS : (z + 1) * K_PASS], in_=rows(w3, z))
         nc.sync.dma_start(dst_sb[:], dst)
-        nc.sync.dma_start(out=w3_raw[:, K_PASS:], in_=rows(w3, 1))
         nc.sync.dma_start(src_sb[:], src)
         second_pick = []
 
@@ -118,7 +121,7 @@ def tile_picked_edgeatt_tanh_p_kernel(tc, x_words, x_scales, w1, w2, w3, offs, s
         banks = {}
 
         def product(i, z, a, b):
-            first, last = [(u, v) for u, v in (Y_BANKS if i == 0 else HALVES) if u <= a < v][0]
+            first, last = [(u, v) for u, v in (Y_BANKS, HALVES, H_BANKS)[i] if u <= a < v][0]
             if (i, first) not in banks:
                 banks[i, first] = psum.tile([P, last - first], F32, name="acc%d_%d" % (i, first))
             nc.tensor.matmul_mx(
@@ -140,7 +143,7 @@ def tile_picked_edgeatt_tanh_p_kernel(tc, x_words, x_scales, w1, w2, w3, offs, s
 
         round_on_scalar(0, 0, w1_raw[0][:])
         quantise(0, 0, 1)
-        for a, b in PIECES:
+        for a, b in Y_BANKS:
             product(0, 0, a, b)
         second_pick.append(sb("second_pick0", [P, PICK_CUT], U32))
         pick_second(0, PICK_CUT)
@@ -149,48 +152,53 @@ def tile_picked_edgeatt_tanh_p_kernel(tc, x_words, x_scales, w1, w2, w3, offs, s
         second_pick.append(sb("second_pick1", [P, S - PICK_CUT], U32, tag="w1_raw1"))
         pick_second(PICK_CUT, LAST_CUT)
         pick_second(LAST_CUT, S)
-        for a, b in PIECES:
+        for a, b in Y_PIECES:
             product(0, 1, a, b)
 
         for z in range(PASSES):
             round_on_scalar(1, z, w2_raw[z][:])
         quantise(1, 0, 2)
-        y = at("y", [P, S], F32, 2048)
+        y = at("y", [P, S], F32, 512)
+        w_grp.append(at("w_grp2", [P, PASSES * K_PASS], BF16, 4608))
+        w3_out = w_grp[2][:].rearrange("p (z c i t) -> p z c t i", z=PASSES, i=4, t=PACK)
+        w3_in = w3_raw[:].rearrange("p (z t c i) -> p z c t i", z=PASSES, i=4, t=PACK)
+        nc.vector.tensor_copy(out=w3_out[:, 0, W3_SCALAR:], in_=w3_in[:, 0, W3_SCALAR:])
         for a, b in Y_BANKS[:2]:
             nc.scalar.copy(out=y[:, a:b], in_=banks[0, a][:])
         for a, b in Y_BANKS[2:]:
             nc.vector.tensor_copy(out=y[:, a:b], in_=banks[0, a][:])
         whole_product(1)
 
+        nc.scalar.copy(out=w3_out[:, :, :W3_SCALAR], in_=w3_in[:, :, :W3_SCALAR])
         y_dst = sb("y_dst", [P, U], F32)
         for a, b in HALVES:
             nc.scalar.activation(y_dst[:, a:b], y[:].indirect(entries(dst_sb, a, b)), COPY)
 
-        nc.vector.tensor_copy(
-            out=w_grp[2][:].rearrange("p (z c i t) -> p z c t i", z=PASSES, i=4, t=PACK),
-            in_=w3_raw[:].rearrange("p (z t c i) -> p z c t i", z=PASSES, i=4, t=PACK),
-        )
+        nc.vector.tensor_copy(out=w3_out[:, 1, W3_SCALAR:], in_=w3_in[:, 1, W3_SCALAR:])
         e = sb("e", [P, S], F32)
         h = sb("h", [P, S], F32)
         nc.vector.tensor_copy(out=e[:, :HALF], in_=banks[1, 0][:])
         quantise(2, 0, 1)
         nc.vector.tensor_copy(out=e[:, HALF:], in_=banks[1, HALF][:])
         quantise(2, 1, 2)
-        for a, b in HALVES:
+        for a, b in PIECES:
             product(2, 0, a, b)
         for a, b in PIECES:
             product(2, 1, a, b)
 
-        pre = sb("pre", [P, U], F32)
+        pre = [sb("pre0", [P, HALF], F32), sb("pre1", [P, HALF], F32, tag="w_code2")]
         gate = sb("gate", [P, U], F32, tag="scale_pick")
         msg = sb("msg", [P, U], F32)
-        for a, b in HALVES:
-            nc.vector.tensor_tensor(pre[:, a:b], e[:].indirect(entries(src_sb, a, b)), y_dst[:, a:b], ADD)
+        nc.vector.tensor_tensor(pre[0][:], e[:].indirect(entries(src_sb, 0, HALF)), y_dst[:, :HALF], ADD)
+        for a, b in H_BANKS[:2]:
             nc.scalar.copy(out=h[:, a:b], in_=banks[2, a][:])
+        for a, b in H_BANKS[2:]:
+            nc.vector.tensor_copy(out=h[:, a:b], in_=banks[2, a][:])
+        nc.vector.tensor_tensor(pre[1][:], e[:].indirect(entries(src_sb, HALF, U)), y_dst[:, HALF:], ADD)
         h_src = {}
         for j, (first, last) in enumerate(PLAIN):
             for a, b in TANH_PIECES[2 * j : 2 * j + 2]:
-                nc.scalar.activation(gate[:, a:b], pre[:, a:b], TANH)
+                nc.scalar.activation(gate[:, a:b], pre[j][:, a % HALF : a % HALF + b - a], TANH)
             h_src[first] = sb("h_src%d" % j, [P, last - first], F32, tag="y_dst" if j else None)
             nc.scalar.activation(h_src[first][:], h[:].indirect(entries(src_sb, first, last)), COPY)
         for a, b in EDGE_PIECES:

@@ -24,13 +24,11 @@ PASSES = K // K_PASS
 GROUP = 16
 HALF = 512
 QUAD = 32
-W3_SCALAR = 8
+W3_SCALAR = 16
 PICK_CUT = 640
 LAST_CUT = 896
 PIECES = ((0, 512), (512, 640), (640, 896), (896, 1024))
-Y_BANKS = ((0, 512), (512, 768), (768, 1024))
-H_BANKS = ((0, 512), (512, 896), (896, 1024))
-Y_PIECES = ((0, 512), (512, 640), (640, 768), (768, 896), (896, 1024))
+BANKS = ((0, 512), (512, 896), (896, 1024))
 HALVES = ((0, 512), (512, 1024))
 PLAIN = ((512, 768), (896, 1024))
 EDGE_PIECES = ((0, 256), (256, 512), (512, 768), (768, 896), (896, 1024))
@@ -64,8 +62,9 @@ def tile_picked_edgeatt_tanh_p_kernel(tc, x_words, x_scales, w1, w2, w3, offs, s
         scale_pick = sb("scale_pick", [P, S], U8)
         word_tab = [at("word_tab0", [P, T], U32, 6144), sb("word_tab1", [P, T], U32)]
         w1_raw = [sb("w1_raw%d" % z, [P, K_PASS], F32) for z in range(PASSES)]
-        w_grp = [sb("w_grp%d" % i, [P, PASSES * K_PASS], BF16) for i in range(2)]
-        w_code = [sb("w_code%d" % i, [P, PASSES * N], U32) for i in range(3)]
+        w_grp = [sb("w_grp%d" % i, [P, PASSES * K_PASS], BF16) for i in range(3)]
+        w_code = [sb("w_code%d" % i, [P, PASSES * N], U32) for i in range(2)]
+        w3_code = [sb("w3_code0", [P, N], U32)]
         w_scale = [sb("w_scale%d" % i, [P, PASSES * N], U8) for i in range(3)]
 
         def load_words(z):
@@ -89,8 +88,13 @@ def tile_picked_edgeatt_tanh_p_kernel(tc, x_words, x_scales, w1, w2, w3, offs, s
                 in_=raw.rearrange("p (t c i) -> p c t i", i=4, t=PACK),
             )
 
+        def codes(i, z0, z1):
+            if i == 2:
+                return w3_code[z0][:]
+            return w_code[i][:, z0 * N : z1 * N]
+
         def quantise(i, z0, z1):
-            nc.vector.quantize_mx(out=w_code[i][:, z0 * N : z1 * N].bitcast(FP8X4), scales=w_scale[i][:, z0 * N : z1 * N], in_=grouped(i, z0, z1))
+            nc.vector.quantize_mx(out=codes(i, z0, z1).bitcast(FP8X4), scales=w_scale[i][:, z0 * N : z1 * N], in_=grouped(i, z0, z1))
 
         nc.vector.tensor_copy(scale_rows[:], scale_tab[:].indirect(offs_sb[:]))
         for q in (0, 2, 1, 3):
@@ -121,12 +125,12 @@ def tile_picked_edgeatt_tanh_p_kernel(tc, x_words, x_scales, w1, w2, w3, offs, s
         banks = {}
 
         def product(i, z, a, b):
-            first, last = [(u, v) for u, v in (Y_BANKS, HALVES, H_BANKS)[i] if u <= a < v][0]
+            first, last = [(u, v) for u, v in (BANKS, HALVES, BANKS)[i] if u <= a < v][0]
             if (i, first) not in banks:
                 banks[i, first] = psum.tile([P, last - first], F32, name="acc%d_%d" % (i, first))
             nc.tensor.matmul_mx(
                 out=banks[i, first][:, a - first : b - first],
-                lhsT=w_code[i][:, z * N : (z + 1) * N].bitcast(FP8X4),
+                lhsT=codes(i, z, z + 1).bitcast(FP8X4),
                 lhsT_scale=w_scale[i][:, z * N : (z + 1) * N],
                 rhs=picked(z, a, b).bitcast(FP8X4),
                 rhs_scale=scale_pick[4 * z :, a:b],
@@ -143,7 +147,7 @@ def tile_picked_edgeatt_tanh_p_kernel(tc, x_words, x_scales, w1, w2, w3, offs, s
 
         round_on_scalar(0, 0, w1_raw[0][:])
         quantise(0, 0, 1)
-        for a, b in Y_BANKS:
+        for a, b in PIECES:
             product(0, 0, a, b)
         second_pick.append(sb("second_pick0", [P, PICK_CUT], U32))
         pick_second(0, PICK_CUT)
@@ -152,47 +156,47 @@ def tile_picked_edgeatt_tanh_p_kernel(tc, x_words, x_scales, w1, w2, w3, offs, s
         second_pick.append(sb("second_pick1", [P, S - PICK_CUT], U32, tag="w1_raw1"))
         pick_second(PICK_CUT, LAST_CUT)
         pick_second(LAST_CUT, S)
-        for a, b in Y_PIECES:
+        for a, b in PIECES:
             product(0, 1, a, b)
 
         for z in range(PASSES):
             round_on_scalar(1, z, w2_raw[z][:])
         quantise(1, 0, 2)
-        y = at("y", [P, S], F32, 512)
-        w_grp.append(at("w_grp2", [P, PASSES * K_PASS], BF16, 4608))
         w3_out = w_grp[2][:].rearrange("p (z c i t) -> p z c t i", z=PASSES, i=4, t=PACK)
         w3_in = w3_raw[:].rearrange("p (z t c i) -> p z c t i", z=PASSES, i=4, t=PACK)
-        nc.vector.tensor_copy(out=w3_out[:, 0, W3_SCALAR:], in_=w3_in[:, 0, W3_SCALAR:])
-        for a, b in Y_BANKS[:2]:
+        nc.scalar.copy(out=w3_out[:, 0, :W3_SCALAR], in_=w3_in[:, 0, :W3_SCALAR])
+        y = at("y", [P, S], F32, 2048)
+        for a, b in BANKS[0::2]:
             nc.scalar.copy(out=y[:, a:b], in_=banks[0, a][:])
-        for a, b in Y_BANKS[2:]:
+        for a, b in BANKS[1:2]:
             nc.vector.tensor_copy(out=y[:, a:b], in_=banks[0, a][:])
         whole_product(1)
 
-        nc.scalar.copy(out=w3_out[:, :, :W3_SCALAR], in_=w3_in[:, :, :W3_SCALAR])
+        nc.scalar.copy(out=w3_out[:, 1, :W3_SCALAR], in_=w3_in[:, 1, :W3_SCALAR])
         y_dst = sb("y_dst", [P, U], F32)
         for a, b in HALVES:
             nc.scalar.activation(y_dst[:, a:b], y[:].indirect(entries(dst_sb, a, b)), COPY)
 
-        nc.vector.tensor_copy(out=w3_out[:, 1, W3_SCALAR:], in_=w3_in[:, 1, W3_SCALAR:])
+        nc.vector.tensor_copy(out=w3_out[:, :, W3_SCALAR:], in_=w3_in[:, :, W3_SCALAR:])
         e = sb("e", [P, S], F32)
         h = sb("h", [P, S], F32)
         nc.vector.tensor_copy(out=e[:, :HALF], in_=banks[1, 0][:])
         quantise(2, 0, 1)
         nc.vector.tensor_copy(out=e[:, HALF:], in_=banks[1, HALF][:])
+        w3_code.append(sb("w3_code1", [P, N], U32, tag="w_code1"))
         quantise(2, 1, 2)
         for a, b in PIECES:
             product(2, 0, a, b)
         for a, b in PIECES:
             product(2, 1, a, b)
 
-        pre = [sb("pre0", [P, HALF], F32), sb("pre1", [P, HALF], F32, tag="w_code2")]
+        pre = [sb("pre0", [P, HALF], F32), sb("pre1", [P, HALF], F32, tag="w_code1")]
         gate = sb("gate", [P, U], F32, tag="scale_pick")
         msg = sb("msg", [P, U], F32)
         nc.vector.tensor_tensor(pre[0][:], e[:].indirect(entries(src_sb, 0, HALF)), y_dst[:, :HALF], ADD)
-        for a, b in H_BANKS[:2]:
+        for a, b in BANKS[:2]:
             nc.scalar.copy(out=h[:, a:b], in_=banks[2, a][:])
-        for a, b in H_BANKS[2:]:
+        for a, b in BANKS[2:]:
             nc.vector.tensor_copy(out=h[:, a:b], in_=banks[2, a][:])
         nc.vector.tensor_tensor(pre[1][:], e[:].indirect(entries(src_sb, HALF, U)), y_dst[:, HALF:], ADD)
         h_src = {}

@@ -24,12 +24,16 @@ PASSES = K // K_PASS
 GROUP = 16
 HALF = 512
 QUAD = 32
+PSUM_BANKS = 8
 W3_SCALAR = 16
 PICK_CUT = 640
 LAST_CUT = 896
 PIECES = ((0, 512), (512, 640), (640, 896), (896, 1024))
-BANKS = ((0, 512), (512, 896), (896, 1024))
 HALVES = ((0, 512), (512, 1024))
+H_BANKS = ((0, 512), (512, 768), (768, 1024))
+H_PIECES = ((0, 512), (512, 640), (640, 768), (768, 1024))
+E_BANKS = ((0, 128), (128, 384), (384, 640), (640, 896), (896, 1024))
+ADD_PIECES = ((0, 256), (256, 512), (512, 1024))
 PLAIN = ((512, 768), (896, 1024))
 EDGE_PIECES = ((0, 256), (256, 512), (512, 768), (768, 896), (896, 1024))
 TANH_PIECES = ((0, 256), (256, 512), (512, 768), (768, 1024))
@@ -125,9 +129,9 @@ def tile_picked_edgeatt_tanh_p_kernel(tc, x_words, x_scales, w1, w2, w3, offs, s
         banks = {}
 
         def product(i, z, a, b):
-            first, last = [(u, v) for u, v in (BANKS, HALVES, BANKS)[i] if u <= a < v][0]
+            first, last = [(u, v) for u, v in (PIECES, E_BANKS, H_BANKS)[i] if u <= a < v][0]
             if (i, first) not in banks:
-                banks[i, first] = psum.tile([P, last - first], F32, name="acc%d_%d" % (i, first))
+                banks[i, first] = psum.tile([P, last - first], F32, name="acc%d_%d" % (i, first), tag="bank%d" % (len(banks) % PSUM_BANKS))
             nc.tensor.matmul_mx(
                 out=banks[i, first][:, a - first : b - first],
                 lhsT=codes(i, z, z + 1).bitcast(FP8X4),
@@ -139,11 +143,9 @@ def tile_picked_edgeatt_tanh_p_kernel(tc, x_words, x_scales, w1, w2, w3, offs, s
             )
 
         def whole_product(i):
-            for first, last in HALVES:
-                product(i, 0, first, last)
-                for a, b in PIECES:
-                    if first <= a < last:
-                        product(i, 1, a, b)
+            for a, b in E_BANKS:
+                for z in range(PASSES):
+                    product(i, z, a, b)
 
         round_on_scalar(0, 0, w1_raw[0][:])
         quantise(0, 0, 1)
@@ -165,38 +167,41 @@ def tile_picked_edgeatt_tanh_p_kernel(tc, x_words, x_scales, w1, w2, w3, offs, s
         w3_out = w_grp[2][:].rearrange("p (z c i t) -> p z c t i", z=PASSES, i=4, t=PACK)
         w3_in = w3_raw[:].rearrange("p (z t c i) -> p z c t i", z=PASSES, i=4, t=PACK)
         nc.scalar.copy(out=w3_out[:, 0, :W3_SCALAR], in_=w3_in[:, 0, :W3_SCALAR])
+        nc.vector.tensor_copy(out=w3_out[:, 0, W3_SCALAR:], in_=w3_in[:, 0, W3_SCALAR:])
         y = at("y", [P, S], F32, 2048)
-        for a, b in BANKS[0::2]:
+        for a, b in PIECES[:1]:
             nc.scalar.copy(out=y[:, a:b], in_=banks[0, a][:])
-        for a, b in BANKS[1:2]:
+        for a, b in PIECES[1:]:
             nc.vector.tensor_copy(out=y[:, a:b], in_=banks[0, a][:])
         whole_product(1)
 
-        nc.scalar.copy(out=w3_out[:, 1, :W3_SCALAR], in_=w3_in[:, 1, :W3_SCALAR])
+        nc.scalar.copy(out=w3_out[:, 1], in_=w3_in[:, 1])
         y_dst = sb("y_dst", [P, U], F32)
-        for a, b in HALVES:
+        for a, b in ADD_PIECES:
             nc.scalar.activation(y_dst[:, a:b], y[:].indirect(entries(dst_sb, a, b)), COPY)
 
-        nc.vector.tensor_copy(out=w3_out[:, :, W3_SCALAR:], in_=w3_in[:, :, W3_SCALAR:])
         e = sb("e", [P, S], F32)
         h = sb("h", [P, S], F32)
-        nc.vector.tensor_copy(out=e[:, :HALF], in_=banks[1, 0][:])
+        for a, b in E_BANKS[:1]:
+            nc.vector.tensor_copy(out=e[:, a:b], in_=banks[1, a][:])
         quantise(2, 0, 1)
-        nc.vector.tensor_copy(out=e[:, HALF:], in_=banks[1, HALF][:])
+        for a, b in E_BANKS[1:]:
+            nc.vector.tensor_copy(out=e[:, a:b], in_=banks[1, a][:])
         w3_code.append(sb("w3_code1", [P, N], U32, tag="w_code1"))
         quantise(2, 1, 2)
-        for a, b in PIECES:
+        for a, b in H_BANKS:
             product(2, 0, a, b)
-        for a, b in PIECES:
+        for a, b in H_PIECES:
             product(2, 1, a, b)
 
         pre = [sb("pre0", [P, HALF], F32), sb("pre1", [P, HALF], F32, tag="w_code1")]
         gate = sb("gate", [P, U], F32, tag="scale_pick")
         msg = sb("msg", [P, U], F32)
-        nc.vector.tensor_tensor(pre[0][:], e[:].indirect(entries(src_sb, 0, HALF)), y_dst[:, :HALF], ADD)
-        for a, b in BANKS[:2]:
+        for a, b in ADD_PIECES[:2]:
+            nc.vector.tensor_tensor(pre[0][:, a:b], e[:].indirect(entries(src_sb, a, b)), y_dst[:, a:b], ADD)
+        for a, b in H_BANKS[:2]:
             nc.scalar.copy(out=h[:, a:b], in_=banks[2, a][:])
-        for a, b in BANKS[2:]:
+        for a, b in H_BANKS[2:]:
             nc.vector.tensor_copy(out=h[:, a:b], in_=banks[2, a][:])
         nc.vector.tensor_tensor(pre[1][:], e[:].indirect(entries(src_sb, HALF, U)), y_dst[:, HALF:], ADD)
         h_src = {}

@@ -28,10 +28,10 @@ PSUM_BANKS = 8
 W3_SCALAR = 16
 PICK_CUT = 640
 LAST_CUT = 896
+Y_CUT = 928
 PIECES = ((0, 512), (512, 640), (640, 896), (896, 1024))
 HALVES = ((0, 512), (512, 1024))
-H_BANKS = ((0, 512), (512, 768), (768, 1024))
-H_PIECES = ((0, 512), (512, 640), (640, 768), (768, 1024))
+H_BANKS = ((0, 512), (512, 896), (896, 1024))
 E_BANKS = ((0, 128), (128, 384), (384, 640), (640, 896), (896, 1024))
 ADD_PIECES = ((0, 256), (256, 512), (512, 1024))
 PLAIN = ((512, 768), (896, 1024))
@@ -176,9 +176,9 @@ def tile_picked_edgeatt_tanh_p_kernel(tc, x_words, x_scales, w1, w2, w3, offs, s
         whole_product(1)
 
         nc.scalar.copy(out=w3_out[:, 1], in_=w3_in[:, 1])
-        y_dst = sb("y_dst", [P, U], F32)
-        for a, b in ADD_PIECES:
-            nc.scalar.activation(y_dst[:, a:b], y[:].indirect(entries(dst_sb, a, b)), COPY)
+        y_dst = [sb("y_dst0", [P, HALF], F32), sb("y_dst1", [P, HALF], F32, tag="w_scale1")]
+        for a, b in ADD_PIECES[:2] + ((HALF, Y_CUT),):
+            nc.scalar.activation(y_dst[a // HALF][:, a % HALF : a % HALF + b - a], y[:].indirect(entries(dst_sb, a, b)), COPY)
 
         e = sb("e", [P, S], F32)
         h = sb("h", [P, S], F32)
@@ -189,26 +189,26 @@ def tile_picked_edgeatt_tanh_p_kernel(tc, x_words, x_scales, w1, w2, w3, offs, s
             nc.vector.tensor_copy(out=e[:, a:b], in_=banks[1, a][:])
         w3_code.append(sb("w3_code1", [P, N], U32, tag="w_code1"))
         quantise(2, 1, 2)
-        for a, b in H_BANKS:
-            product(2, 0, a, b)
-        for a, b in H_PIECES:
-            product(2, 1, a, b)
+        nc.vector.tensor_copy(y_dst[1][:, Y_CUT - HALF :], y[:].indirect(entries(dst_sb, Y_CUT, U)))
+        for z in range(PASSES):
+            for a, b in PIECES:
+                product(2, z, a, b)
 
         pre = [sb("pre0", [P, HALF], F32), sb("pre1", [P, HALF], F32, tag="w_code1")]
         gate = sb("gate", [P, U], F32, tag="scale_pick")
         msg = sb("msg", [P, U], F32)
         for a, b in ADD_PIECES[:2]:
-            nc.vector.tensor_tensor(pre[0][:, a:b], e[:].indirect(entries(src_sb, a, b)), y_dst[:, a:b], ADD)
+            nc.vector.tensor_tensor(pre[0][:, a:b], e[:].indirect(entries(src_sb, a, b)), y_dst[0][:, a:b], ADD)
         for a, b in H_BANKS[:2]:
             nc.scalar.copy(out=h[:, a:b], in_=banks[2, a][:])
         for a, b in H_BANKS[2:]:
             nc.vector.tensor_copy(out=h[:, a:b], in_=banks[2, a][:])
-        nc.vector.tensor_tensor(pre[1][:], e[:].indirect(entries(src_sb, HALF, U)), y_dst[:, HALF:], ADD)
+        nc.vector.tensor_tensor(pre[1][:], e[:].indirect(entries(src_sb, HALF, U)), y_dst[1][:], ADD)
         h_src = {}
         for j, (first, last) in enumerate(PLAIN):
             for a, b in TANH_PIECES[2 * j : 2 * j + 2]:
                 nc.scalar.activation(gate[:, a:b], pre[j][:, a % HALF : a % HALF + b - a], TANH)
-            h_src[first] = sb("h_src%d" % j, [P, last - first], F32, tag="y_dst" if j else None)
+            h_src[first] = sb("h_src%d" % j, [P, last - first], F32, tag="w_scale1" if j else None)
             nc.scalar.activation(h_src[first][:], h[:].indirect(entries(src_sb, first, last)), COPY)
         for a, b in EDGE_PIECES:
             if a not in h_src:

@@ -25,14 +25,13 @@ GROUP = 16
 HALF = 512
 QUAD = 32
 PSUM_BANKS = 8
-W3_SCALAR = 16
+ALIGN = 64
 PICK_CUT = 640
 LAST_CUT = 896
-Y_CUT = 928
 PIECES = ((0, 512), (512, 640), (640, 896), (896, 1024))
-HALVES = ((0, 512), (512, 1024))
-H_BANKS = ((0, 512), (512, 896), (896, 1024))
+Y_BANKS = ((0, 512), (512, 896), (896, 1024))
 E_BANKS = ((0, 128), (128, 384), (384, 640), (640, 896), (896, 1024))
+H_BANKS = ((0, 512), (512, 1024))
 ADD_PIECES = ((0, 256), (256, 512), (512, 1024))
 PLAIN = ((512, 768), (896, 1024))
 EDGE_PIECES = ((0, 256), (256, 512), (512, 768), (768, 896), (896, 1024))
@@ -47,10 +46,10 @@ def tile_picked_edgeatt_tanh_p_kernel(tc, x_words, x_scales, w1, w2, w3, offs, s
         psum = ctx.enter_context(tc.psum_pool(name="psum", bufs=1))
 
         def sb(name, shape, dtype, tag=None):
-            return keep.tile(shape, dtype, name=name, tag=tag or name, align_bytes=64)
+            return keep.tile(shape, dtype, name=name, tag=tag or name, align_bytes=ALIGN)
 
         def at(name, shape, dtype, offset):
-            return reuse.tile(shape, dtype, name=name, align_bytes=64, offset=offset)
+            return reuse.tile(shape, dtype, name=name, align_bytes=ALIGN, offset=offset)
 
         def entries(lst, a, b):
             return lst[:, a // GROUP : b // GROUP]
@@ -66,9 +65,8 @@ def tile_picked_edgeatt_tanh_p_kernel(tc, x_words, x_scales, w1, w2, w3, offs, s
         scale_pick = sb("scale_pick", [P, S], U8)
         word_tab = [at("word_tab0", [P, T], U32, 6144), sb("word_tab1", [P, T], U32)]
         w1_raw = [sb("w1_raw%d" % z, [P, K_PASS], F32) for z in range(PASSES)]
-        w_grp = [sb("w_grp%d" % i, [P, PASSES * K_PASS], BF16) for i in range(3)]
+        w_grp = [sb("w_grp%d" % i, [P, PASSES * K_PASS], BF16) for i in range(2)]
         w_code = [sb("w_code%d" % i, [P, PASSES * N], U32) for i in range(2)]
-        w3_code = [sb("w3_code0", [P, N], U32)]
         w_scale = [sb("w_scale%d" % i, [P, PASSES * N], U8) for i in range(3)]
 
         def load_words(z):
@@ -86,19 +84,14 @@ def tile_picked_edgeatt_tanh_p_kernel(tc, x_words, x_scales, w1, w2, w3, offs, s
         def grouped(i, z0, z1):
             return w_grp[i][:, z0 * K_PASS : z1 * K_PASS]
 
-        def round_on_scalar(i, z, raw):
-            nc.scalar.copy(
-                out=grouped(i, z, z + 1).rearrange("p (c i t) -> p c t i", i=4, t=PACK),
-                in_=raw.rearrange("p (t c i) -> p c t i", i=4, t=PACK),
-            )
+        def walk_out(i, z):
+            return grouped(i, z, z + 1).rearrange("p (c i t) -> p c t i", i=4, t=PACK)
 
-        def codes(i, z0, z1):
-            if i == 2:
-                return w3_code[z0][:]
-            return w_code[i][:, z0 * N : z1 * N]
+        def walk_in(raw):
+            return raw.rearrange("p (t c i) -> p c t i", i=4, t=PACK)
 
         def quantise(i, z0, z1):
-            nc.vector.quantize_mx(out=codes(i, z0, z1).bitcast(FP8X4), scales=w_scale[i][:, z0 * N : z1 * N], in_=grouped(i, z0, z1))
+            nc.vector.quantize_mx(out=w_code[i][:, z0 * N : z1 * N].bitcast(FP8X4), scales=w_scale[i][:, z0 * N : z1 * N], in_=grouped(i, z0, z1))
 
         nc.vector.tensor_copy(scale_rows[:], scale_tab[:].indirect(offs_sb[:]))
         for q in (0, 2, 1, 3):
@@ -109,9 +102,9 @@ def tile_picked_edgeatt_tanh_p_kernel(tc, x_words, x_scales, w1, w2, w3, offs, s
             nc.sync.dma_start(out=w2_raw[z][:], in_=rows(w2, z))
         first_pick = sb("first_pick", [P, S], U32)
         nc.vector.tensor_copy(first_pick[:], word_tab[0][:].indirect(offs_sb[:]))
-        w3_raw = at("w3_raw", [P, PASSES * K_PASS], F32, 8192)
+        w3_raw = [at("w3_raw%d" % z, [P, K_PASS], F32, 8192 + 2048 * z) for z in range(PASSES)]
         for z in range(PASSES):
-            nc.sync.dma_start(out=w3_raw[:, z * K_PASS : (z + 1) * K_PASS], in_=rows(w3, z))
+            nc.sync.dma_start(out=w3_raw[z][:], in_=rows(w3, z))
         nc.sync.dma_start(dst_sb[:], dst)
         nc.sync.dma_start(src_sb[:], src)
         second_pick = []
@@ -129,12 +122,12 @@ def tile_picked_edgeatt_tanh_p_kernel(tc, x_words, x_scales, w1, w2, w3, offs, s
         banks = {}
 
         def product(i, z, a, b):
-            first, last = [(u, v) for u, v in (PIECES, E_BANKS, H_BANKS)[i] if u <= a < v][0]
+            first, last = [(u, v) for u, v in (Y_BANKS, E_BANKS, H_BANKS)[i] if u <= a < v][0]
             if (i, first) not in banks:
                 banks[i, first] = psum.tile([P, last - first], F32, name="acc%d_%d" % (i, first), tag="bank%d" % (len(banks) % PSUM_BANKS))
             nc.tensor.matmul_mx(
                 out=banks[i, first][:, a - first : b - first],
-                lhsT=codes(i, z, z + 1).bitcast(FP8X4),
+                lhsT=w_code[i][:, z * N : (z + 1) * N].bitcast(FP8X4),
                 lhsT_scale=w_scale[i][:, z * N : (z + 1) * N],
                 rhs=picked(z, a, b).bitcast(FP8X4),
                 rhs_scale=scale_pick[4 * z :, a:b],
@@ -142,18 +135,13 @@ def tile_picked_edgeatt_tanh_p_kernel(tc, x_words, x_scales, w1, w2, w3, offs, s
                 stop=(z == PASSES - 1 and b == last),
             )
 
-        def whole_product(i):
-            for a, b in E_BANKS:
-                for z in range(PASSES):
-                    product(i, z, a, b)
-
-        round_on_scalar(0, 0, w1_raw[0][:])
+        nc.scalar.copy(out=walk_out(0, 0), in_=walk_in(w1_raw[0][:]))
         quantise(0, 0, 1)
         for a, b in PIECES:
             product(0, 0, a, b)
         second_pick.append(sb("second_pick0", [P, PICK_CUT], U32))
         pick_second(0, PICK_CUT)
-        round_on_scalar(0, 1, w1_raw[1][:])
+        nc.scalar.copy(out=walk_out(0, 1), in_=walk_in(w1_raw[1][:]))
         quantise(0, 1, 2)
         second_pick.append(sb("second_pick1", [P, S - PICK_CUT], U32, tag="w1_raw1"))
         pick_second(PICK_CUT, LAST_CUT)
@@ -162,47 +150,42 @@ def tile_picked_edgeatt_tanh_p_kernel(tc, x_words, x_scales, w1, w2, w3, offs, s
             product(0, 1, a, b)
 
         for z in range(PASSES):
-            round_on_scalar(1, z, w2_raw[z][:])
+            nc.scalar.copy(out=walk_out(1, z), in_=walk_in(w2_raw[z][:]))
         quantise(1, 0, 2)
-        w3_out = w_grp[2][:].rearrange("p (z c i t) -> p z c t i", z=PASSES, i=4, t=PACK)
-        w3_in = w3_raw[:].rearrange("p (z t c i) -> p z c t i", z=PASSES, i=4, t=PACK)
-        nc.scalar.copy(out=w3_out[:, 0, :W3_SCALAR], in_=w3_in[:, 0, :W3_SCALAR])
-        nc.vector.tensor_copy(out=w3_out[:, 0, W3_SCALAR:], in_=w3_in[:, 0, W3_SCALAR:])
-        y = at("y", [P, S], F32, 2048)
-        for a, b in PIECES[:1]:
+        w_grp.append(at("w_grp2", [P, PASSES * K_PASS], BF16, 5120))
+        for z in range(PASSES):
+            nc.vector.tensor_copy(out=walk_out(2, z), in_=walk_in(w3_raw[z][:]))
+        y = at("y", [P, S], F32, 1024)
+        for a, b in Y_BANKS[:2]:
             nc.scalar.copy(out=y[:, a:b], in_=banks[0, a][:])
-        for a, b in PIECES[1:]:
+        for a, b in Y_BANKS[2:]:
             nc.vector.tensor_copy(out=y[:, a:b], in_=banks[0, a][:])
-        whole_product(1)
-
-        nc.scalar.copy(out=w3_out[:, 1], in_=w3_in[:, 1])
-        y_dst = [sb("y_dst0", [P, HALF], F32), sb("y_dst1", [P, HALF], F32, tag="w_scale1")]
-        for a, b in ADD_PIECES[:2] + ((HALF, Y_CUT),):
-            nc.scalar.activation(y_dst[a // HALF][:, a % HALF : a % HALF + b - a], y[:].indirect(entries(dst_sb, a, b)), COPY)
-
-        e = sb("e", [P, S], F32)
-        h = sb("h", [P, S], F32)
-        for a, b in E_BANKS[:1]:
-            nc.vector.tensor_copy(out=e[:, a:b], in_=banks[1, a][:])
-        quantise(2, 0, 1)
-        for a, b in E_BANKS[1:]:
-            nc.vector.tensor_copy(out=e[:, a:b], in_=banks[1, a][:])
-        w3_code.append(sb("w3_code1", [P, N], U32, tag="w_code1"))
-        quantise(2, 1, 2)
-        nc.vector.tensor_copy(y_dst[1][:, Y_CUT - HALF :], y[:].indirect(entries(dst_sb, Y_CUT, U)))
+        for a, b in E_BANKS:
+            for z in range(PASSES):
+                product(1, z, a, b)
+        w_code.append(sb("w_code2", [P, PASSES * N], U32, tag="w_code0"))
+        for z in range(PASSES):
+            quantise(2, z, z + 1)
         for z in range(PASSES):
             for a, b in PIECES:
                 product(2, z, a, b)
 
-        pre = [sb("pre0", [P, HALF], F32), sb("pre1", [P, HALF], F32, tag="w_code1")]
+        y_dst = [sb("y_dst0", [P, HALF], F32), sb("y_dst1", [P, HALF], F32, tag="w_scale1")]
+        for a, b in ADD_PIECES[:2]:
+            nc.vector.tensor_copy(y_dst[0][:, a:b], y[:].indirect(entries(dst_sb, a, b)))
+        e = sb("e", [P, S], F32)
+        h = sb("h", [P, S], F32)
+        for a, b in E_BANKS:
+            nc.scalar.copy(out=e[:, a:b], in_=banks[1, a][:])
+        nc.scalar.activation(y_dst[1][:], y[:].indirect(entries(dst_sb, HALF, U)), COPY)
+
+        pre = [sb("pre0", [P, HALF], F32), sb("pre1", [P, HALF], F32)]
         gate = sb("gate", [P, U], F32, tag="scale_pick")
         msg = sb("msg", [P, U], F32)
         for a, b in ADD_PIECES[:2]:
             nc.vector.tensor_tensor(pre[0][:, a:b], e[:].indirect(entries(src_sb, a, b)), y_dst[0][:, a:b], ADD)
-        for a, b in H_BANKS[:2]:
+        for a, b in H_BANKS:
             nc.scalar.copy(out=h[:, a:b], in_=banks[2, a][:])
-        for a, b in H_BANKS[2:]:
-            nc.vector.tensor_copy(out=h[:, a:b], in_=banks[2, a][:])
         nc.vector.tensor_tensor(pre[1][:], e[:].indirect(entries(src_sb, HALF, U)), y_dst[1][:], ADD)
         h_src = {}
         for j, (first, last) in enumerate(PLAIN):

@@ -25,7 +25,7 @@ GROUP = 16
 HALF = 512
 QUAD = 32
 PSUM_BANKS = 8
-ALIGN = 64
+ALIGN = 256
 PICK_CUT = 640
 LAST_CUT = 896
 PIECES = ((0, 512), (512, 640), (640, 896), (896, 1024))

@@ -30,7 +30,8 @@ PICK_CUT = 640
 LAST_CUT = 896
 PIECES = ((0, 512), (512, 640), (640, 896), (896, 1024))
 Y_BANKS = ((0, 512), (512, 896), (896, 1024))
-E_BANKS = ((0, 128), (128, 384), (384, 640), (640, 896), (896, 1024))
+E_PIECES = ((0, 128), (128, 384), (384, 640), (640, 896), (896, 1024))
+E_BANKS = ((0, 384), (384, 640), (640, 1024))
 H_BANKS = ((0, 512), (512, 1024))
 ADD_PIECES = ((0, 256), (256, 512), (512, 1024))
 PLAIN = ((512, 768), (896, 1024))
@@ -160,9 +161,11 @@ def tile_picked_edgeatt_tanh_p_kernel(tc, x_words, x_scales, w1, w2, w3, offs, s
             nc.scalar.copy(out=y[:, a:b], in_=banks[0, a][:])
         for a, b in Y_BANKS[2:]:
             nc.vector.tensor_copy(out=y[:, a:b], in_=banks[0, a][:])
-        for a, b in E_BANKS:
+        for first, last in E_BANKS:
             for z in range(PASSES):
-                product(1, z, a, b)
+                for a, b in E_PIECES:
+                    if first <= a < last:
+                        product(1, z, a, b)
         w_code.append(sb("w_code2", [P, PASSES * N], U32, tag="w_code0"))
         for z in range(PASSES):
             quantise(2, z, z + 1)

from contextlib import ExitStack

import concourse.mybir as mybir

K, T, S, N, U = 1024, 2048, 1024, 128, 1024
FLOPS = 3 * 2 * K * N * S

F32 = mybir.dt.float32
BF16 = mybir.dt.bfloat16
I32 = mybir.dt.int32
U32 = mybir.dt.uint32
U16 = mybir.dt.uint16
U8 = mybir.dt.uint8
FP8X4 = mybir.dt.float8_e4m3fn_x4
ADD = mybir.AluOpType.add
MULT = mybir.AluOpType.mult
TANH = mybir.ActivationFunctionType.Tanh
COPY = mybir.ActivationFunctionType.Copy

P = 128
PACK = 4
K_PASS = P * PACK
PASSES = K // K_PASS
GROUP = 16
HALF = 512
QUAD = 32
PSUM_BANKS = 8
ALIGN = 256
PICK_CUT = 640
LAST_CUT = 896
PIECES = ((0, 512), (512, 640), (640, 896), (896, 1024))
Y_BANKS = ((0, 512), (512, 896), (896, 1024))
E_PIECES = ((0, 128), (128, 384), (384, 640), (640, 896), (896, 1024))
E_BANKS = ((0, 384), (384, 640), (640, 1024))
H_BANKS = ((0, 512), (512, 1024))
ADD_PIECES = ((0, 256), (256, 512), (512, 1024))
PLAIN = ((512, 768), (896, 1024))
EDGE_PIECES = ((0, 256), (256, 512), (512, 768), (768, 896), (896, 1024))
TANH_PIECES = ((0, 256), (256, 512), (512, 768), (768, 1024))


def tile_picked_edgeatt_tanh_p_kernel(tc, x_words, x_scales, w1, w2, w3, offs, src, dst, out):
    nc = tc.nc
    with ExitStack() as ctx:
        keep = ctx.enter_context(tc.tile_pool(name="keep", bufs=1))
        reuse = ctx.enter_context(tc.tile_pool(name="reuse", bufs=1))
        psum = ctx.enter_context(tc.psum_pool(name="psum", bufs=1))

        def sb(name, shape, dtype, tag=None):
            return keep.tile(shape, dtype, name=name, tag=tag or name, align_bytes=ALIGN)

        def at(name, shape, dtype, offset):
            return reuse.tile(shape, dtype, name=name, align_bytes=ALIGN, offset=offset)

        def entries(lst, a, b):
            return lst[:, a // GROUP : b // GROUP]

        def rows(w, z):
            return w[z * K_PASS : (z + 1) * K_PASS, :].rearrange("(p j) m -> p (j m)", j=PACK)

        offs_sb = keep.tile([P, S // GROUP], U16, name="offs_sb")
        src_sb = keep.tile([P, U // GROUP], U16, name="src_sb")
        dst_sb = keep.tile([P, U // GROUP], U16, name="dst_sb")
        scale_tab = at("scale_tab", [P, T], U8, 3072)
        scale_rows = sb("scale_rows", [P, S], U8)
        scale_pick = sb("scale_pick", [P, S], U8)
        word_tab = [at("word_tab0", [P, T], U32, 6144), sb("word_tab1", [P, T], U32)]
        w1_raw = [sb("w1_raw%d" % z, [P, K_PASS], F32) for z in range(PASSES)]
        w_grp = [sb("w_grp%d" % i, [P, PASSES * K_PASS], BF16) for i in range(2)]
        w_code = [sb("w_code%d" % i, [P, PASSES * N], U32) for i in range(2)]
        w_scale = [sb("w_scale%d" % i, [P, PASSES * N], U8) for i in range(3)]

        def load_words(z):
            nc.sync.dma_start(out=word_tab[z][:].bitcast(I32), in_=x_words[z].rearrange("p n t -> p (n t)").bitcast(I32))

        nc.vector.memset(scale_tab[QUAD : 2 * QUAD, :].bitcast(I32), 0)
        nc.vector.memset(scale_tab[2 * QUAD : P, :].bitcast(I32), 0)
        for z in reversed(range(PASSES)):
            nc.sync.dma_start(out=scale_tab[16 * z : 16 * z + 16, :].bitcast(I32), in_=x_scales[z].rearrange("(q i) t -> i q t", q=4).bitcast(I32))
        nc.sync.dma_start(offs_sb[:], offs)
        load_words(0)
        nc.sync.dma_start(out=w1_raw[0][:], in_=rows(w1, 0))
        load_words(1)

        def grouped(i, z0, z1):
            return w_grp[i][:, z0 * K_PASS : z1 * K_PASS]

        def walk_out(i, z):
            return grouped(i, z, z + 1).rearrange("p (c i t) -> p c t i", i=4, t=PACK)

        def walk_in(raw):
            return raw.rearrange("p (t c i) -> p c t i", i=4, t=PACK)

        def quantise(i, z0, z1):
            nc.vector.quantize_mx(out=w_code[i][:, z0 * N : z1 * N].bitcast(FP8X4), scales=w_scale[i][:, z0 * N : z1 * N], in_=grouped(i, z0, z1))

        nc.vector.tensor_copy(scale_rows[:], scale_tab[:].indirect(offs_sb[:]))
        for q in (0, 2, 1, 3):
            nc.sync.dma_start(out=scale_pick[32 * q : 32 * q + 8, :].bitcast(I32), in_=scale_rows[q:QUAD:4, :].bitcast(I32))
        nc.sync.dma_start(out=w1_raw[1][:], in_=rows(w1, 1))
        w2_raw = [at("w2_raw%d" % z, [P, K_PASS], F32, 2048 * (z + 1)) for z in range(PASSES)]
        for z in range(PASSES):
            nc.sync.dma_start(out=w2_raw[z][:], in_=rows(w2, z))
        first_pick = sb("first_pick", [P, S], U32)
        nc.vector.tensor_copy(first_pick[:], word_tab[0][:].indirect(offs_sb[:]))
        w3_raw = [at("w3_raw%d" % z, [P, K_PASS], F32, 8192 + 2048 * z) for z in range(PASSES)]
        for z in range(PASSES):
            nc.sync.dma_start(out=w3_raw[z][:], in_=rows(w3, z))
        nc.sync.dma_start(dst_sb[:], dst)
        nc.sync.dma_start(src_sb[:], src)
        second_pick = []

        def picked(z, a, b):
            if z == 0:
                return first_pick[:, a:b]
            if a < PICK_CUT:
                return second_pick[0][:, a:b]
            return second_pick[1][:, a - PICK_CUT : b - PICK_CUT]

        def pick_second(a, b):
            nc.vector.tensor_copy(picked(1, a, b), word_tab[1][:].indirect(entries(offs_sb, a, b)))

        banks = {}

        def product(i, z, a, b):
            first, last = [(u, v) for u, v in (Y_BANKS, E_BANKS, H_BANKS)[i] if u <= a < v][0]
            if (i, first) not in banks:
                banks[i, first] = psum.tile([P, last - first], F32, name="acc%d_%d" % (i, first), tag="bank%d" % (len(banks) % PSUM_BANKS))
            nc.tensor.matmul_mx(
                out=banks[i, first][:, a - first : b - first],
                lhsT=w_code[i][:, z * N : (z + 1) * N].bitcast(FP8X4),
                lhsT_scale=w_scale[i][:, z * N : (z + 1) * N],
                rhs=picked(z, a, b).bitcast(FP8X4),
                rhs_scale=scale_pick[4 * z :, a:b],
                start=(z == 0 and a == first),
                stop=(z == PASSES - 1 and b == last),
            )

        nc.scalar.copy(out=walk_out(0, 0), in_=walk_in(w1_raw[0][:]))
        quantise(0, 0, 1)
        for a, b in PIECES:
            product(0, 0, a, b)
        second_pick.append(sb("second_pick0", [P, PICK_CUT], U32))
        pick_second(0, PICK_CUT)
        nc.scalar.copy(out=walk_out(0, 1), in_=walk_in(w1_raw[1][:]))
        quantise(0, 1, 2)
        second_pick.append(sb("second_pick1", [P, S - PICK_CUT], U32, tag="w1_raw1"))
        pick_second(PICK_CUT, LAST_CUT)
        pick_second(LAST_CUT, S)
        for a, b in PIECES:
            product(0, 1, a, b)

        for z in range(PASSES):
            nc.scalar.copy(out=walk_out(1, z), in_=walk_in(w2_raw[z][:]))
        quantise(1, 0, 2)
        w_grp.append(at("w_grp2", [P, PASSES * K_PASS], BF16, 5120))
        for z in range(PASSES):
            nc.vector.tensor_copy(out=walk_out(2, z), in_=walk_in(w3_raw[z][:]))
        y = at("y", [P, S], F32, 1024)
        for a, b in Y_BANKS[:2]:
            nc.scalar.copy(out=y[:, a:b], in_=banks[0, a][:])
        for a, b in Y_BANKS[2:]:
            nc.vector.tensor_copy(out=y[:, a:b], in_=banks[0, a][:])
        for first, last in E_BANKS:
            for z in range(PASSES):
                for a, b in E_PIECES:
                    if first <= a < last:
                        product(1, z, a, b)
        w_code.append(sb("w_code2", [P, PASSES * N], U32, tag="w_code0"))
        for z in range(PASSES):
            quantise(2, z, z + 1)
        for z in range(PASSES):
            for a, b in PIECES:
                product(2, z, a, b)

        y_dst = [sb("y_dst0", [P, HALF], F32), sb("y_dst1", [P, HALF], F32, tag="w_scale1")]
        for a, b in ADD_PIECES[:2]:
            nc.vector.tensor_copy(y_dst[0][:, a:b], y[:].indirect(entries(dst_sb, a, b)))
        e = sb("e", [P, S], F32)
        h = sb("h", [P, S], F32)
        for a, b in E_BANKS:
            nc.scalar.copy(out=e[:, a:b], in_=banks[1, a][:])
        nc.scalar.activation(y_dst[1][:], y[:].indirect(entries(dst_sb, HALF, U)), COPY)

        pre = [sb("pre0", [P, HALF], F32), sb("pre1", [P, HALF], F32)]
        gate = sb("gate", [P, U], F32, tag="scale_pick")
        msg = sb("msg", [P, U], F32)
        for a, b in ADD_PIECES[:2]:
            nc.vector.tensor_tensor(pre[0][:, a:b], e[:].indirect(entries(src_sb, a, b)), y_dst[0][:, a:b], ADD)
        for a, b in H_BANKS:
            nc.scalar.copy(out=h[:, a:b], in_=banks[2, a][:])
        nc.vector.tensor_tensor(pre[1][:], e[:].indirect(entries(src_sb, HALF, U)), y_dst[1][:], ADD)
        h_src = {}
        for j, (first, last) in enumerate(PLAIN):
            for a, b in TANH_PIECES[2 * j : 2 * j + 2]:
                nc.scalar.activation(gate[:, a:b], pre[j][:, a % HALF : a % HALF + b - a], TANH)
            h_src[first] = sb("h_src%d" % j, [P, last - first], F32, tag="w_scale1" if j else None)
            nc.scalar.activation(h_src[first][:], h[:].indirect(entries(src_sb, first, last)), COPY)
        for a, b in EDGE_PIECES:
            if a not in h_src:
                nc.vector.tensor_tensor(msg[:, a:b], h[:].indirect(entries(src_sb, a, b)), gate[:, a:b], MULT)
            else:
                nc.vector.tensor_tensor(msg[:, a:b], h_src[a][:], gate[:, a:b], MULT)
            nc.sync.dma_start(out=out[:, a:b], in_=msg[:, a:b])
